import numpy as np, ml_dtypes
CORES = [6,15,38,47]
N = 4
import mx_ref
BF = ml_dtypes.bfloat16
def tile(rs):
    return np.stack(rs, axis=2).reshape(128, -1).astype(BF)
def pick(q, e):
    c = np.concatenate([q[0].reshape(128, -1, 4), np.zeros((128, 1, 4), np.uint8)], axis=1); s = np.concatenate([q[1], np.ones((16, 1), np.uint8)], axis=1)
    return (np.ascontiguousarray(c[:, e].reshape(128, -1)), np.ascontiguousarray(s[:, e]))
def join(*qs):
    return (np.concatenate([q[0] for q in qs], axis=1), np.concatenate([q[1] for q in qs], axis=1))
def put(q, e, v):
    c, s = q[0].reshape(128, -1, 4).copy(), q[1].copy(); c[:, e] = v[0].reshape(128, -1, 4); s[:, e] = v[1]
    return (c.reshape(128, -1), s)
def pk(c, s):
    return (np.ascontiguousarray(c), mx_ref.live(s))
def emit(q):
    return q[0], q[1]
def packed(v, rng):
    q = [mx_ref.quantize(np.ascontiguousarray(v[r])) for r in range(N)]
    return np.stack([a for a, b in q]), np.stack([mx_ref.plane(b, rng) for a, b in q])
def values_of_codes():
    e, c = np.zeros((128, 128, 4), np.float32), np.zeros((128, 2, 4), np.uint8)
    e[np.arange(128), np.arange(128), 0] = 1
    c[:127, :, 0] = np.arange(256).reshape(2, 128).T[:127]
    return mx_ref.matmul(mx_ref.quantize(e.reshape(128, 512).astype(BF)), (c.reshape(128, 8), np.full((16, 2), 127, np.uint8))).T.reshape(-1).astype(np.float64)
CODE_VALUE, SCALE_VALUE = values_of_codes(), 2.0 ** (np.arange(256) - 127.0)
def decode(q):
    return (CODE_VALUE[q[0]].reshape(16, 8, -1, 4) * SCALE_VALUE[q[1]][:, None, :, None] + 0.0).reshape(128, -1).astype(np.float32)
def f(rng, *shape):
    return mx_ref.flush((rng.standard_normal(shape, dtype=np.float32) * np.exp2(rng.integers(-2, 3, shape[:-1] + (1,)))).astype(BF))
def wide(rng, *shape, cols=0):
    v = rng.standard_normal(shape, dtype=np.float32) * np.exp2(rng.integers(-12, 13, shape)).astype(np.float32)
    if cols: v *= np.repeat(np.exp2(rng.integers(-cols, cols + 1, shape[:-2] + (1, shape[-1] // 4))) * (rng.random(shape[:-2] + (1, shape[-1] // 4)) > 0.0625), 4, axis=-1).astype(np.float32)
    return mx_ref.flush(v.astype(BF))
C, H = 288, 144
MASK = [1, 2, 3]
def numbers_of(rng):
    return {"x": np.array(f(rng, N, 128, 4 * C)), "u": np.array(f(rng, N, 128, 512)), "v": np.array(f(rng, N, 128, 512))}
def layers(rng, still=[]):
    w = np.array(mx_ref.flush((np.clip(f(rng, N, 128, 2048).astype(np.float32), -4, 4) * np.float32(0.125)).astype(BF))).reshape(N, 8, 16, 4, 8, 16, 4)
    for i in still: w[:, :, :, :, :, i] = 0
    return w
def weights(rng, w):
    c, p = packed(np.ascontiguousarray(w).reshape(N, 128, 2048), rng)
    return {"wc": c, "ws": p}
def setup_inputs(rng):
    return {**numbers_of(rng), **weights(rng, layers(rng))}
def setup_inputs_ties(rng):
    d = numbers_of(rng)
    o = rng.permutation(N)
    x = d["x"].reshape(N, 8, 16, C, 4)
    k = rng.integers(0, 3, (N, 8, C)) - 4 * (o % 2)[:, None, None]
    k[o == 2] = np.arange(8)[:, None]
    x[:, :, 0] = 0
    x[:, :, 0, :, 0] = k.astype(np.float32).astype(BF)
    z = 1 + 32 * rng.permutation(C // 32)[np.arange(C) // 32] + rng.permutation(32)[np.arange(C) % 32]
    z = 4 * z[None, :] + ((np.arange(8) + int(rng.choice([2, 4, 6]))) % 8 // 2)[:, None]
    for r in range(N):
        if o[r] == 3: x[r, :, 0] = (-((z[:, :, None] >> (3 * np.arange(4))) & 7)).astype(np.float32).astype(BF)
    n = (N, 8, 8, C, 4)
    a = (129 + 2 * rng.integers(0, 64, n)) * np.exp2(-7.0 - rng.integers(8, 15, n)) * (rng.integers(0, 2, n) * 2.0 - 1.0)
    a[:, :, 0, :, 0] = 1.96875
    a = a * np.exp2(1.0 * rng.integers(-2, 3, (N, 8, 1, C, 1)))
    x[:, :, 8:] = a.astype(np.float32).astype(BF)
    u = d["u"].reshape(N, 128, 128, 4)
    u[:, :, ::16] = 0
    for r in range(N):
        for h in range(0, 128, 16):
            u[r, h, h, 0] = 0.0 if o[r] == 0 else -1.0 if o[r] == 1 else 1.0
            if o[r] == 3: u[r, h, h] = np.exp2(3.0 * np.arange(4)).astype(np.float32).astype(BF)
    return {"x": x.reshape(N, 128, 4 * C), "u": u.reshape(N, 128, 512), "v": d["v"], **weights(rng, layers(rng, [0] + [*range(8, 16)]))}
def setup_inputs_near(rng):
    d = numbers_of(rng)
    x = d["x"].astype(np.float32).reshape(N, 8, 16, C, 4)
    x[:, :, 0] = 0
    x[:, :, 8:] = 0
    u = d["u"].reshape(N, 128, 128, 4)
    u[:, :, ::16] = 0
    o = rng.permutation(N) % 4
    for r in range(N):
        s = rng.integers(0, 16, (8, C, 1))
        if o[r] < 3: x[r, :, 8] = ((s >> np.arange(4)) & 1) * np.exp2(np.arange(4) - 23.0)
        if o[r] < 2:
            x[r, :, 0, :, 0] = rng.integers(0, 2, (8, C)) * 2.0 - 1.0
            x[r, :, 11, :, 0] = 2.0 ** -10
        if o[r] == 2:
            e = rng.permutation(8)
            x[r, e[0], 0, :, 0] = 1.0
            x[r, e[1], 0, :, 0] = -1.0
        if o[r] == 3:
            x[r, :4, 10, :, 0] = rng.choice([1.0, 2.0], (4, C)) * 2.0 ** -30
            x[r, 4:, 10, :, 0] = rng.choice([1.125, 2.0], (4, C)) * 2.0 ** -30
            t = rng.permutation(C)[:C // 4]
            z = rng.integers(0, 2, (8, C // 4)) * 0.25
            c = np.where(np.arange(8) < 4, 1.0, 1.125)[:, None]
            x[r][:, 10, t, 0] = (c + z) * 2.0 ** -30
            x[r][:, 12, t, 0] = (c - z - 2.125) * 2.0 ** -30
        k = 1.0 if o[r] == 0 else 2.0 ** -30
        for h in range(0, 128, 16):
            u[r, h, h, 0] = 1.0 if o[r] == 2 else k
            u[r, h + 8, h] = k
            u[r, h + 11, h, 0] = k
            u[r, h + 10, h, 0] = k if o[r] < 3 else k * 1.25 if h < 64 else k * 1.125
            u[r, h + 12, h, 0] = 0.0 if o[r] < 3 else k * 1.125 if h < 64 else k * 1.25
    return {"x": x.reshape(N, 128, 4 * C).astype(BF), "u": u.reshape(N, 128, 512), "v": d["v"], **weights(rng, layers(rng, [0] + [*range(8, 16)]))}
def setup_inputs_huge(rng):
    d = numbers_of(rng)
    o = rng.permutation(N) % 2
    c = rng.integers(0, 2, (N, 1, 1, C, 1)) * 2.0 - 1.0
    c[o == 0] = -1.0
    x = (0.6 + 0.08 * rng.random((N, 8, 16, C, 4))) * 2.0 ** 30 * c
    a = 2.0 ** 30 * (1.0 - 0.1 * rng.random((N, 128, 8, 4)))
    a[o == 1] *= rng.choice([-1.0, 1.0], (N // 2, 1, 8, 1))
    u = d["u"].reshape(N, 128, 128, 4)
    u[:, :, ::16] = a.astype(np.float32).astype(BF)
    w = rng.integers(1, 3, (N, 8, 16, 4, 8, 16, 4)) * 2.0 ** -9 * rng.choice([-1.0, 1.0], (N, 1, 1, 4, 8, 16, 1))
    return {"x": x.astype(np.float32).reshape(N, 128, 4 * C).astype(BF), "u": u.reshape(N, 128, 512), "v": d["v"], **weights(rng, w.astype(np.float32).astype(BF))}
def setup_inputs_ends(rng):
    d = numbers_of(rng)
    o = rng.permutation(N) % 4
    most, least = 255.0 * 2.0 ** 22, 2.0 ** -30
    x = np.full((N, 8, C), least)
    u = d["u"].reshape(N, 8, 16, 128, 4)
    v = rng.choice([-1.0, 1.0], (N, 128, 512))
    for r in range(N):
        a = np.ones((8, 16, 8, 4)) * (2.0 ** -30 if o[r] == 2 else 2.0 ** 30)
        if o[r] == 0:
            x[r] = -most
            for g in rng.permutation(8)[:4]: a[:, :, g] *= rng.choice([0.5, 1.0], (8, 16, 4))
        else: a *= rng.choice([-1.0, 1.0], (8, 1, 8, 1))
        if o[r] == 1: x[r] = most * rng.choice([-1.0, 1.0], (1, C))
        if o[r] == 3: x[r] = np.where(rng.random((8, C)) < 0.5, least, most * rng.choice([-1.0, 1.0], (8, C)))
        u[r][:, :, ::16] = a.astype(np.float32).astype(BF)
        v[r] *= 2.0 ** 30 if o[r] % 2 == 0 else 2.0 ** -30
    x = x[:, :, None, :, None] * np.ones((1, 1, 16, 1, 4))
    w = rng.choice([-1.0, 1.0], (N, 8, 16, 1, 8, 2, 1, 4)) * np.full((1, 1, 1, 4, 1, 1, 8, 1), least)
    return {"x": x.astype(np.float32).reshape(N, 128, 4 * C).astype(BF), "u": u.reshape(N, 128, 512), "v": v.astype(np.float32).astype(BF), **weights(rng, w.astype(np.float32).astype(BF))}
def setup_inputs_spread(rng):
    d = setup_inputs(rng)
    d["x"] = wide(rng, N, 128, 4 * C, cols=2)
    return d
def check_inputs(d):
    b = []
    for k in ("x", "u", "v"):
        a = np.abs(d[k].astype(np.float32))
        if not (np.isfinite(a).all() and ((a == 0) | (a >= 2.0 ** -30) & (a <= 2.0 ** 30)).all()): b.append("a value of " + k)
    none, least, most = [emit(mx_ref.quantize(np.full((128, 16), k, np.float32).astype(BF)))[1][0, 0] for k in (0.0, 2.0 ** -30, 2.0 ** 30)]
    top = 0.0
    for r in range(N):
        if ((d["wc"][r] == 0x7F) | (d["wc"][r] == 0xFF)).any(): b.append("wc: a code that is no number")
        s = mx_ref.live(d["ws"][r])
        if ((s != none) & ((s < least) | (s > most))).any(): b.append("ws: a scale out of range")
        top = max(top, float(np.abs(decode(pk(d["wc"][r], d["ws"][r]))).max()))
    if not float(np.abs(d["x"].astype(np.float32)).max()) * (1.0 + 32.0 * top) * (1.0 + 32.0 * top) * (1.0 + 32.0 * top) <= 2.0 ** 30: b.append("x and W: too large together")
    return b
def reference(x, u, v, wc, ws):
    qu = [mx_ref.quantize(u[r]) for r in range(N)]
    lay = [pk(wc[r], ws[r]) for r in range(N)]
    now = [x[r] for r in range(N)]
    place = np.zeros((N, 8 * C), np.int64)
    for m in MASK:
        seats, made = [], []
        for r in range(N):
            q = mx_ref.quantize(now[r])
            own = decode(q).astype(BF).reshape(8, 16, C, 4)
            s = mx_ref.matmul(qu[r], q)[::16] + np.float32(0.0)
            o = np.argsort(-s.reshape(-1), kind="stable")
            place[r, o] = np.arange(8 * C)
            t = own[o // C, :, o % C].reshape(C, 8, 16, 4).transpose(1, 2, 0, 3)
            seats.append(mx_ref.quantize(np.ascontiguousarray(t).reshape(128, 4 * C)))
        for r in range(N):
            q = join(pick(seats[r ^ m], np.arange(H)), pick(seats[r], np.arange(H, C)))
            a = decode(q)
            t = tile([np.maximum(mx_ref.matmul(pick(lay[r], np.arange(128 * b, 128 * b + 128)), q), np.float32(0.0)) * np.float32(0.03125) + a[:, b::4] for b in range(4)])
            n = place[r].reshape(8, C)
            home = t.reshape(8, 16, C, 4)[n % 8, :, n // 8]
            made.append(np.ascontiguousarray(home.transpose(0, 2, 1, 3)).reshape(128, 4 * C))
        now = made
    y, pl = np.zeros((N, 128, C), np.float32), np.zeros((N, 8, C), np.float32)
    oc, osc = np.zeros((N, 128, 4 * C), np.uint8), np.zeros((N, 16, C), np.uint8)
    for r in range(N):
        q = mx_ref.quantize(now[r])
        y[r] = mx_ref.matmul(mx_ref.quantize(v[r]), q)
        pl[r] = place[r].reshape(8, C)
        oc[r], osc[r] = emit(q)
    return {"y": y, "pl": pl, "oc": oc, "osc": osc}

@@ -1,0 +1,438 @@
+from concourse.mybir import dt, AluOpType, AxisListType, ActivationFunctionType
+
+OP = AluOpType
+ACT = ActivationFunctionType
+C = 288
+H = 144
+BIG = 1.0e29
+EPS = 2.0 ** -24 + 2.0 ** -40
+DELTA = 2.0 ** -100
+MASKS = [1, 2, 3]
+
+SCRATCH = {}
+for _t, _s in (
+        ("float32", "pf 8 it0 320 it1 320 it2 320 neg8 8 own8 8 offadd 144 offt 144 offe 144 offo 144 msel 144 mselt 144 cvf 288 ssb 288 sr 2304 dm 288 d1 144 d2 72 d3 36 sc 24 r17 18 qf 18 pof 18 sort 288 spm 16 spv 4 sp8 16 wm 272 wn 72 wt 72 off32 144 off33 144 ntf 32 ntt 32 en 504 rt 1152 ysb 288"),
+        ("int32", "pi 8 ii 256 wli 64 rr 18 q32 18 nt 32 ph 96"),
+        ("uint16", "clist 18 ul 72 wl 64 posl 18 off 144 phl 18 tl 72 hl 72"),
+        ("bfloat16", "gm 8 mk16 288 mk17 288 tri 288 mk272 272 cval 288 ones 64 zer 2304 ef 4096 ob 512 zb 1024 zz 1792 xt 1152 ut 512 vt 512 et 288 ml 5760 mc 2304 mf 2304 iw0 2304 iw1 2304 iw2 2304 itr 2304 fw 2304 ow 1152 tt 1152 o2 1152 tw 2304"),
+        ("mx", "ef 1024 ob 128 zb 256 zz 448 u 128 v 128 up 1152 w 512 wl 1024 x 288 ml 1440 mc 576 mf 576 tb 144 ta0 144 ta1 144 ta2 144 lc0 144 lc1 144 lc2 144")):
+    _s = _s.split()
+    for _n, _w in zip(_s[::2], _s[1::2]):
+        if _t == "mx":
+            SCRATCH[_n + "_q"] = ("sbuf", [128, int(_w)], "float8_e4m3fn_x4")
+            SCRATCH[_n + "_s"] = ("sbuf", [128, int(_w)], "uint8")
+        else:
+            SCRATCH[_n] = ("sbuf", [128, int(_w)], _t)
+for _m in range(8):
+    SCRATCH["p%d" % _m] = ("psum", [128, 512], "float32")
+
+SEMAPHORES = "sv sa st sg lx lu lw ls lv z0 z1 z2 z3 z4 outd arr0 arr1 arr2 sent0 sent1 sent2".split()
+
+
+def rank_program(g, core, T, topo):
+    rank = T.rank_of(core)
+    if rank is None:
+        return
+    wait = {"V": g.vector.wait_ge, "S": g.scalar.wait_ge, "T": g.tensor.wait_ge, "G": g.wait_ge, "Y": g.sync.wait_ge}
+    own = {"V": "sv", "S": "sa", "T": "st", "G": "sg"}
+    total, snaps, hist = {}, {}, {}
+    known = {q: {} for q in "VSTGYR"}
+
+    def view(name, c0, c1, st=1, p0=0, p1=128):
+        if p0 == 0 and p1 == 128:
+            ap = T[name][:, c0:c1] if st == 1 else T[name][:, c0:c1:st]
+        else:
+            ap = T[name][p0:p1, c0:c1] if st == 1 else T[name][p0:p1, c0:c1:st]
+        return (name, p0, p1, c0, c1, st, ap)
+
+    def clash(a, b):
+        if a[1] >= b[2] or b[1] >= a[2] or a[3] >= b[4] or b[3] >= a[4]:
+            return False
+        return not (a[5] == b[5] and a[5] > 1 and (a[3] - b[3]) % a[5])
+
+    def covers(a, b):
+        return a[1] <= b[1] and a[2] >= b[2] and a[3] <= b[3] and a[4] >= b[4] and (a[5] == 1 or (a[5] == b[5] and (a[3] - b[3]) % a[5] == 0))
+
+    def settle(q, reads, writes, group=False):
+        need = {}
+        for kind, vs in (("r", reads), ("w", writes)):
+            for v in vs:
+                bank = SCRATCH[v[0]][0] == "psum"
+                for (k2, q2, v2, sem, val) in hist.get(v[0], []):
+                    if q2 == q and q in "VSTG":
+                        if k2 == "r" or (group and bank) or not clash(v, v2):
+                            continue
+                    elif not bank and ((kind == "r" and k2 == "r") or not clash(v, v2)):
+                        continue
+                    need[sem] = max(need.get(sem, 0), val)
+        kn = known[q]
+        for sem, val in sorted(need.items(), key=lambda e: -e[1]):
+            if kn.get(sem, 0) >= val:
+                continue
+            wait[q](T.sem[sem], val)
+            kn[sem] = val
+            for s2, v2 in snaps.get((sem, val), {}).items():
+                kn[s2] = max(kn.get(s2, 0), v2)
+
+    def note(q, sem, val, reads, writes):
+        snaps[(sem, val)] = dict(known[q])
+        for k, vs in (("w", writes), ("r", reads)):
+            for v in vs:
+                h = hist.setdefault(v[0], [])
+                if k == "w":
+                    h[:] = [e for e in h if not covers(v, e[2])]
+                else:
+                    h[:] = [e for e in h if not (e[0] == "r" and e[1] == q and q in "VSTG" and covers(v, e[2]))]
+                h.append((k, q, v, sem, val))
+
+    def run(q, call, reads, writes, group=False):
+        settle(q, reads, writes, group)
+        sem = own[q]
+        total[sem] = total.get(sem, 0) + 1
+        call().then_inc(T.sem[sem], 1)
+        note(q, sem, total[sem], reads, writes)
+
+    def dma(sem, out, in_, reads, writes):
+        settle("Y", reads, writes)
+        total[sem] = total.get(sem, 0) + 16
+        g.sync.dma_start(out, in_).then_inc(T.sem[sem], 16)
+        note("Y", sem, total[sem], reads, writes)
+
+    def ap(x):
+        return x[6] if isinstance(x, tuple) else x
+
+    def rd(*xs):
+        return [x for x in xs if isinstance(x, tuple)]
+
+    def ts(out, a, s1, op0, s2=None, op1=None):
+        if op1 is None:
+            run("V", lambda: g.vector.tensor_scalar(out[6], a[6], ap(s1), None, op0), rd(a, s1), [out])
+        else:
+            run("V", lambda: g.vector.tensor_scalar(out[6], a[6], ap(s1), ap(s2), op0, op1), rd(a, s1, s2), [out])
+
+    def tt(out, a, b, op):
+        run("V", lambda: g.vector.tensor_tensor(out[6], a[6], b[6], op), [a, b], [out])
+
+    def tc(out, a):
+        run("V", lambda: g.vector.tensor_copy(out[6], a[6]), [a], [out])
+
+    def fill(out, c):
+        run("V", lambda: g.vector.memset(out[6], c), [], [out])
+
+    def gather(out, win, off):
+        run("V", lambda: g.vector.tensor_copy(out[6], win[6].indirect(off[6])), [win, off], [out])
+
+    def fused(out, win, off, b, op):
+        run("V", lambda: g.vector.tensor_tensor(out[6], win[6].indirect(off[6]), b[6], op), [win, off, b], [out])
+
+    def scatter(win, off, a):
+        run("V", lambda: g.vector.tensor_copy(win[6].indirect(off[6]), a[6]), [a, off], [win])
+
+    def turn(out, a):
+        run("V", lambda: g.vector.transpose(out[6], a[6]), [a], [out])
+
+    def quant(n, a, c0, c1):
+        o, p = view(n + "_q", c0, c1), view(n + "_s", c0, c1)
+        run("V", lambda: g.vector.quantize_mx(o[6], p[6], a[6]), [a], [o, p])
+
+    def act(out, a, f=ACT.Copy, scale=1.0):
+        if scale == 1.0:
+            run("S", lambda: g.scalar.activation(out[6], a[6], f), [a], [out])
+        else:
+            run("S", lambda: g.scalar.activation(out[6], a[6], f, scale=scale), [a], [out])
+
+    def iota(out, pattern, base=0, cm=0, f=True):
+        if f:
+            run("G", lambda: g.iota(out[6], pattern, base, cm, allow_small_or_imprecise_dtypes=True), [], [out])
+        else:
+            run("G", lambda: g.iota(out[6], pattern, base, cm), [], [out])
+
+    def mm(bank, n, l, l0, r, r0, start=True, stop=True):
+        o = view("p%d" % bank, 0, n)
+        lq, ls, rq, rs = view(l + "_q", l0, l0 + 128), view(l + "_s", l0, l0 + 128), view(r + "_q", r0, r0 + n), view(r + "_s", r0, r0 + n)
+        run("T", lambda: g.tensor.matmul_mx(o[6], lq[6], ls[6], rq[6], rs[6], start, stop), [lq, ls, rq, rs], [o], group=not start)
+
+    def ps(bank, c0, c1, st=1):
+        return view("p%d" % bank, c0, c1, st)
+
+    def pick(dst, src, n0, n1, w, off):
+        o, i, o2, i2 = view(dst + "_q", n0, n1), view(src + "_q", 0, w), view(dst + "_s", n0, n1), view(src + "_s", 0, w)
+        run("V", lambda: g.vector.tensor_copy(o[6].bitcast(dt.uint32), i[6].bitcast(dt.uint32).indirect(off[6])), [i, off], [o])
+        run("S", lambda: g.scalar.activation(o2[6], i2[6].indirect(off[6]), ACT.Copy), [i2, off], [o2])
+
+    for sem, name, src, w in (("lx", "xt", T.x, 1152), ("lu", "ut", T.u, 512)):
+        dma(sem, T[name][:, 0:w], src[:], [], [view(name, 0, w)])
+    dma("lw", T.w_q[:, 0:512].bitcast(dt.uint8), T.wc[:], [], [view("w_q", 0, 512)])
+    dma("ls", T.w_s[:, 0:512], T.ws[:], [], [view("w_s", 0, 512)])
+    dma("lv", T.vt[:, 0:512], T.v[:], [], [view("vt", 0, 512)])
+    pcol = [view("pf", k, k + 1) for k in range(8)]
+    pi = [view("pi", k, k + 1) for k in range(8)]
+    iota(pi[0], [[0, 1]], 0, 1, f=False)
+    iota(view("ii", 0, 8), [[16, 8]], f=False)
+    iota(view("ii", 8, 72), [[16, 8], [0, 8]], f=False)
+    iota(view("it0", 0, 288), [[0, 18], [1, 16]])
+    iota(view("it1", 144, 152), [[1, 8]])
+    iota(view("ii", 72, 90), [[1, 18]], f=False)
+    iota(view("it1", 0, 144), [[1, 8], [0, 18]])
+    iota(view("it2", 0, 272), [[1, 16], [0, 17]])
+    iota(view("cvf", 0, 288), [[1, 288]], -144, 0)
+    iota(view("it1", 160, 304), [[0, 36], [1, 4]])
+    iota(view("ii", 96, 160), [[16, 8], [128, 4], [0, 2]], f=False)
+
+    fill(view("zer", 0, 2304), 0.0)
+    for sem, name, c0, c1 in (("z0", "ef", 0, 2304), ("z1", "ef", 2304, 4096), ("z2", "iw0", 0, 2304), ("z3", "iw1", 0, 2304), ("z4", "iw2", 0, 2304)):
+        dma(sem, T[name][:, c0:c1], T.zer[:, 0:c1 - c0], [view("zer", 0, c1 - c0)], [view(name, c0, c1)])
+    fill(view("ones", 0, 64), 1.0)
+    ts(pi[1], pi[0], 15, OP.bitwise_and)
+    ts(pi[2], pi[0], 4, OP.logical_shift_right)
+    ts(pi[3], pi[0], 4, OP.logical_shift_right, 1, OP.bitwise_and)
+    ts(pi[4], pi[0], 5, OP.logical_shift_right)
+    ts(pi[5], pi[0], 15, OP.bitwise_and, 2, OP.logical_shift_right)
+    tc(view("ul", 0, 72), view("ii", 0, 72))
+    for k in range(3):
+        tc(pcol[k], pi[k + 1])
+    ts(pcol[3], pi[4], 576, OP.mult, 144, OP.add)
+    ts(pcol[4], pi[4], 576, OP.mult, 432, OP.add)
+    tc(pcol[5], pi[5])
+    ts(pi[6], pi[5], 1, OP.bitwise_and)
+    ts(pcol[6], pi[6], 4096.0, OP.mult)
+    ts(pcol[7], pi[6], -4096.0, OP.mult, 4096.0, OP.add)
+    ts(view("mk16", 0, 288), view("it0", 0, 288), pcol[0], OP.is_equal)
+    tc(view("clist", 0, 18), view("ii", 72, 90))
+    fill(view("sc", 16, 24), 0.0)
+    for h in range(8):
+        for t in range(4):
+            o, i = view("ef", 512 * h + 128 * t + t, 512 * h + 128 * t + 128, 4), view("ones", 0, 32)
+            run("G", lambda: g.affine_select(o[6], i[6], [[0, 2], [-1, 16]], OP.is_equal, 0.0, -16 * h, 1), [i], [o])
+    quant("u", view("ut", 0, 512), 0, 128)
+    pick("up", "u", 0, 128, 128, view("ul", 0, 8))
+
+    def constants_1():
+        pick("up", "u", 128, 1152, 128, view("ul", 8, 72))
+        ts(view("gm", 0, 8), view("it1", 144, 152), pcol[1], OP.is_equal)
+        ts(view("tri", 0, 288), view("it0", 0, 288), pcol[0], OP.is_gt)
+        fill(view("ml", 4 * 1152 + 3, 5760, 4), 0.0)
+        for k in range(8):
+            ts(view("ob", 64 * k, 64 * k + 64), view("ones", 0, 64), view("gm", k, k + 1), OP.mult)
+        quant("ob", view("ob", 0, 512), 0, 128)
+
+    def constants_2():
+        ts(view("mk17", 0, 288), view("mk16", 0, 288), 17.0, OP.mult)
+        ts(view("neg8", 0, 8), view("it1", 144, 152), pcol[1], OP.is_lt, -1.0, OP.mult)
+        ts(view("own8", 0, 8), view("it1", 144, 152), pcol[1], OP.is_equal, -BIG, OP.mult)
+        ts(view("offadd", 0, 144), view("it1", 0, 144), pcol[1], OP.is_lt, 24.0, OP.mult)
+        ts(view("offt", 0, 144), view("it1", 0, 144), pcol[1], OP.is_equal, 48.0, OP.mult)
+        tt(view("offadd", 0, 144), view("offadd", 0, 144), view("offt", 0, 144), OP.add)
+        ts(view("offe", 0, 144), view("offadd", 0, 144), pcol[6], OP.subtract)
+        ts(view("offo", 0, 144), view("offadd", 0, 144), pcol[7], OP.subtract)
+        ts(view("mk272", 0, 272), view("it2", 0, 272), pcol[0], OP.is_equal)
+        fill(view("zb", 0, 1024), 0.0)
+        for z in range(4):
+            for b in range(4):
+                tc(view("zb", 512 * (z // 2) + 16 * z + 5 * b, 512 * (z // 2) + 512, 64), view("gm", 0, 8))
+        quant("zb", view("zb", 0, 1024), 0, 256)
+        fill(view("zz", 0, 1792), 0.0)
+        for w in range(2):
+            for b in range(4):
+                fill(view("zz", 896 * w + 384 + 5 * b, 896 * w + 512, 16), 16.0 if w else 1.0)
+        quant("zz", view("zz", 0, 1792), 0, 448)
+        fill(view("wn", 0, 48), 0.0)
+        fill(view("wn", 48, 72), -BIG)
+        ts(view("msel", 0, 144), view("it1", 160, 304), pcol[5], OP.is_equal)
+        ts(view("mselt", 0, 144), view("msel", 0, 144), pcol[2], OP.mult)
+        tt(view("mselt", 0, 72), view("msel", 0, 72), view("mselt", 0, 72), OP.subtract)
+        tc(view("cval", 0, 288), view("cvf", 0, 288))
+        fill(view("cval", 144, 145), 0.25)
+        quant("ef", view("ef", 0, 2048), 0, 512)
+        quant("ef", view("ef", 2048, 4096), 512, 1024)
+
+    def constants_3():
+        ts(view("wli", 0, 64), view("ii", 96, 160), pcol[0], OP.add)
+        tc(view("wl", 0, 64), view("wli", 0, 64))
+        pick("wl", "w", 0, 1024, 512, view("wl", 0, 64))
+        quant("v", view("vt", 0, 512), 0, 128)
+
+    def tree(v, out):
+        tt(view("d1", 0, 144), view(v, 0, 288, 2), view(v, 1, 288, 2), OP.add)
+        tt(view("d2", 0, 72), view("d1", 0, 144, 2), view("d1", 1, 144, 2), OP.add)
+        tt(view("d3", 0, 36), view("d2", 0, 72, 2), view("d2", 1, 72, 2), OP.add)
+        tt(out, view("d3", 0, 36, 2), view("d3", 1, 36, 2), OP.add)
+
+    def places(rnd):
+        mm(0, C, "up", 0, "x", 0)
+        tt(view("dm", 0, 288), ps(0, 0, 288), view("mk16", 0, 288), OP.mult)
+        tc(view("ssb", 0, 288), ps(0, 0, 288))
+        tree("dm", view("sc", 0, 18))
+        if rnd == 0:
+            constants_1()
+        for k in range(8):
+            mm(2 + k % 4, C, "up", 128 + 128 * k, "x", 0)
+            act(view("sr", 288 * k, 288 * k + 288), ps(2 + k % 4, 0, 288))
+        fused(view("et", 0, 288), view("sc", 0, 24), view("clist", 0, 18), view("ssb", 0, 288), OP.is_equal)
+        tt(view("ml", 4 * 1152 + 2, 5760, 4), view("et", 0, 288), view("tri", 0, 288), OP.mult)
+        for al in range(5):
+            for a in range(4 * al, min(18, 4 * al + 4)):
+                c = 16 * a + 16
+                ts(view("ml", 1152 * al + a % 4, 1152 * al + 4 * c, 4), view("ssb", 0, c), view("sc", a, a + 1), OP.is_lt)
+                if c < C:
+                    ts(view("ml", 1152 * al + 4 * c + a % 4, 1152 * al + 1152, 4), view("ssb", c, C), view("sc", a, a + 1), OP.is_le)
+            quant("ml", view("ml", 1152 * al, 1152 * al + 1152), 288 * al, 288 * al + 288)
+            mm(1, C, "ob", 0, "ml", 288 * al, al == 0, al == 4)
+        if rnd == 0:
+            constants_2()
+        for k in range(8):
+            mm(2 + k % 4, C, "ef", 128 * k, "x", 0)
+            act(view("fw", 288 * k, 288 * k + 288), ps(2 + k % 4, 0, 288))
+        tt(view("dm", 0, 288), ps(1, 0, 288), view("mk17", 0, 288), OP.mult)
+        r17 = view("r17", 0, 18)
+        tree("dm", r17)
+        ts(view("q32", 0, 18), r17, 1.0 / 289.0, OP.mult, -136.0 / 289.0, OP.add)
+        ts(view("qf", 0, 18), view("q32", 0, 18), -288.0, OP.mult)
+        tt(view("pof", 0, 18), r17, view("qf", 0, 18), OP.add)
+        tc(view("posl", 0, 18), view("pof", 0, 18))
+        scatter(view("sort", 0, 288), view("posl", 0, 18), view("ssb", 0, 288))
+        sm = view("spm", 0, 16)
+        tt(sm, view("sort", 272, 288), view("mk16", 0, 16), OP.mult)
+        sp, spa, dec = view("spv", 0, 1), view("spv", 1, 2), view("spv", 2, 3)
+        run("V", lambda: g.vector.tensor_reduce(sp[6], sm[6], AxisListType.X, OP.add), [sm], [sp])
+        run("V", lambda: g.vector.tensor_reduce(spa[6], sm[6], AxisListType.X, OP.add, apply_absolute_value=True), [sm], [spa])
+        ts(dec, spa, EPS, OP.mult, DELTA, OP.add)
+        ts(view("sp8", 0, 8), view("neg8", 0, 8), dec, OP.mult, sp, OP.add)
+        tt(view("sp8", 8, 16), view("sp8", 0, 8), view("own8", 0, 8), OP.add)
+        for hf in range(2):
+            for gr in range(4 * hf, 4 * hf + 4):
+                ts(view("mc", 288 * gr, 288 * gr + 288), view("sr", 288 * gr, 288 * gr + 288), view("sp8", 8 + gr, 9 + gr), OP.is_le)
+            quant("mc", view("mc", 1152 * hf, 1152 * hf + 1152), 288 * hf, 288 * hf + 288)
+            for z in range(2):
+                mm(6 + hf, 286, "zb", 128 * z, "mc", 288 * hf + 2 * z, z == 0, z == 1)
+        for k in range(4):
+            for w in range(2):
+                mm(1, H, "zz", 224 * w + 96 - 32 * k, "mc", 144 * k, k == 0 and w == 0, False)
+        tt(view("wm", 0, 272), view("sort", 0, 272), view("mk272", 0, 272), OP.mult)
+        for n in (136, 68, 34):
+            tt(view("wm", 0, n), view("wm", 0, n), view("wm", n, 2 * n), OP.add)
+        tt(view("wn", 0, 17), view("wm", 0, 17), view("wm", 17, 34), OP.add)
+        ts(view("wt", 0, 17), view("wn", 0, 17), EPS, OP.mult, -DELTA, OP.add)
+        ts(view("wt", 24, 41), view("wn", 0, 17), -EPS, OP.mult, -DELTA, OP.add)
+        tt(view("wt", 48, 65), view("wt", 0, 17), view("wt", 24, 41), OP.min)
+        tt(view("wn", 24, 41), view("wn", 0, 17), view("wt", 48, 65), OP.add)
+        ts(view("rr", 0, 18), r17, 1.0 / 17.0, OP.mult)
+        for hf in range(2):
+            c0, c1 = 72 * hf, 72 * hf + 72
+            o, o2 = view("off32", c0, c1), view("off33", c0, c1)
+            tt(o, ps(6 + hf, 0, 286, 4), view("offe", c0, c1), OP.add)
+            tt(o2, ps(6 + hf, 1, 286, 4), view("offo", c0, c1), OP.add)
+            tt(o, o, o2, OP.max)
+            tc(view("off", c0, c1), o)
+        for k in range(4):
+            o = view("mf", 576 * k, 576 * k + 576)
+            fused(o, view("wn", 0, 72), view("off", 36 * k, 36 * k + 36), view("sr", 576 * k, 576 * k + 576), OP.is_ge)
+            quant("mf", o, 144 * k, 144 * k + 144)
+            mm(1, H, "zz", 96 - 32 * k, "mf", 144 * k, False, k == 3)
+        tt(view("wm", 0, 144), ps(1, 0, 144), view("mselt", 0, 144), OP.mult)
+        tt(view("d2", 0, 72), view("wm", 0, 72), view("wm", 72, 144), OP.add)
+        tt(view("d3", 0, 36), view("d2", 0, 72, 2), view("d2", 1, 72, 2), OP.add)
+        tt(view("pof", 0, 18), view("d3", 0, 36, 2), view("d3", 1, 36, 2), OP.add)
+        tt(view("nt", 0, 18), view("pof", 0, 18), view("rr", 0, 18), OP.add)
+
+    def seats(rnd):
+        n = view("nt", 0, 18)
+        ph = [view("ph", 18 * k, 18 * k + 18) for k in range(5)]
+        ts(ph[0], n, 1, OP.logical_shift_right)
+        ts(ph[1], n, 1, OP.logical_shift_right, 65520, OP.bitwise_and)
+        ts(ph[2], n, 16, OP.mult)
+        ts(ph[3], ph[0], -31, OP.mult)
+        tt(ph[2], ph[2], ph[1], OP.add)
+        tt(ph[4], ph[2], ph[3], OP.add)
+        tc(view("phl", 0, 18), ph[4])
+        iw = view("iw%d" % rnd, 0, 2304)
+        scatter(iw, view("phl", 0, 18), view("cval", 0, 288))
+        turn(view("itr", 0, 2304), iw)
+        e = [(72 * k, 72 * k + 72) for k in range(7)]
+        i0, i1 = view("itr", 0, 2304, 32), view("itr", 16, 2304, 32)
+        ts(view("en", *e[0]), i0, 0.0, OP.not_equal, pcol[3], OP.mult)
+        ts(view("en", *e[1]), i1, 0.0, OP.not_equal, pcol[4], OP.mult)
+        tt(view("en", *e[2]), view("en", *e[0]), i0, OP.add)
+        tt(view("en", *e[3]), view("en", *e[1]), i1, OP.add)
+        tt(view("en", *e[4]), view("en", *e[2]), view("en", *e[3]), OP.add)
+        tc(view("en", *e[5], p1=64), view("en", *e[4], p0=64))
+        tt(view("en", *e[6], p1=64), view("en", *e[4], p1=64), view("en", *e[5], p1=64), OP.add)
+        tc(view("en", *e[0], p1=32), view("en", *e[6], p0=32, p1=64))
+        tt(view("en", *e[1], p1=32), view("en", *e[6], p1=32), view("en", *e[0], p1=32), OP.add)
+        for t in range(4):
+            tc(view("tl", 0, 72, p0=32 * t, p1=32 * t + 32), view("en", *e[1], p1=32))
+
+    def native(dst, dc, src, sc, n, sst, order):
+        for k, (q, t) in enumerate(order):
+            o = view(dst, dc + t, dc + 4 * n, 4, 32 * q, 32 * q + 32)
+            if sst == 1:
+                i = view(src, sc + n * q, sc + n * q + n, 1, 32 * t, 32 * t + 32)
+            else:
+                i = view(src, sc + q, sc + 4 * n, 4, 32 * t, 32 * t + 32)
+            if k % 3 == 2:
+                act(o, i)
+            else:
+                tc(o, i)
+
+    ALL = [(q, t) for q in range(4) for t in range(4)]
+
+    def layer(src, half):
+        for h in range(8):
+            a, b = (2 * h) % 8, (2 * h + 1) % 8
+            mm(a, H, "wl", 128 * h, src, 0)
+            mm(b, H, "ef", 128 * h, src, 0)
+            r = view("rt", 144 * h, 144 * h + 144)
+            act(r, ps(a, 0, 144), ACT.Relu, 0.03125)
+            tt(view("tw", 1152 * half + h, 1152 * half + 1152, 8), ps(b, 0, 144), r, OP.add)
+
+    for rnd in range(3):
+        quant("x", view("xt", 0, 1152), 0, 288)
+        places(rnd)
+        seats(rnd)
+        ta, lc = "ta%d" % rnd, "lc%d" % rnd
+        gather(view("ow", 0, 576), view("fw", 0, 2304), view("tl", 0, 36))
+        native("tt", 0, "ow", 0, 144, 4, ALL)
+        quant(ta, view("tt", 0, 576), 0, 144)
+        dst = T.cores[rank ^ MASKS[rnd]]
+        rid, pid = topo.addr(dst)[0], topo.addr(dst)[1]
+        mask, ne = topo.mask(core, dst), len(topo.engines(core, dst))
+        settle("G", [view(ta + "_q", 0, 144), view(ta + "_s", 0, 144)], [])
+        arr, sent = "arr%d" % rnd, "sent%d" % rnd
+        g.remote_dma(T[lc + "_q"][:, 0:144].bitcast(dt.uint8), T[ta + "_q"][:, 0:144].bitcast(dt.uint8), T.sem[arr], T.sem[sent], pid, rid, mask)
+        g.remote_dma(T[lc + "_s"][:, 0:144], T[ta + "_s"][:, 0:144], T.sem[arr], T.sem[sent], pid, rid, mask)
+        total[arr] = total[sent] = 2 * ne
+        note("R", arr, 2 * ne, [], [view(lc + "_q", 0, 144), view(lc + "_s", 0, 144)])
+        gather(view("ow", 576, 1152), view("fw", 0, 2304), view("tl", 36, 72))
+        native("tt", 576, "ow", 576, 144, 4, ALL)
+        quant("tb", view("tt", 576, 1152), 0, 144)
+        if rnd == 0:
+            constants_3()
+        for q in range(4):
+            tc(view("hl", 18 * q, 18 * q + 18, p1=32), view("nt", 0, 18, p0=32 * q, p1=32 * q + 32))
+        for t in range(1, 4):
+            tc(view("hl", 0, 72, p0=32 * t, p1=32 * t + 32), view("hl", 0, 72, p1=32))
+        layer("tb", 1)
+        if rnd == 2:
+            fill(view("ntf", 18, 32), 0.0)
+            tc(view("ntf", 0, 18), view("nt", 0, 18))
+            turn(view("ntt", 0, 32), view("ntf", 0, 32))
+            for gr in range(8):
+                v = view("ntt", 16 * (gr % 2), 16 * (gr % 2) + 16, 1, 32 * (gr // 2), 32 * (gr // 2) + 18)
+                dma("outd", T.pl[gr:gr + 1, :], v[6], [v], [])
+        layer(lc, 0)
+        for k in range(2):
+            gather(view("o2", 576 * k, 576 * k + 576), view("tw", 0, 2304), view("hl", 36 * k, 36 * k + 36))
+            native("xt", 0, "o2", 0, 288, 1, ALL[8 * k:8 * k + 8])
+    quant("x", view("xt", 0, 1152), 0, 288)
+    mm(0, C, "v", 0, "x", 0)
+    v = view("x_q", 0, 288)
+    dma("outd", T.oc[:], v[6].bitcast(dt.uint8), [v], [])
+    for k in range(4):
+        v = view("x_s", 0, 288, 1, 32 * k, 32 * k + 4)
+        dma("outd", T.osc[4 * k:4 * k + 4, :], v[6], [v], [])
+    tc(view("ysb", 0, 288), ps(0, 0, 288))
+    v = view("ysb", 0, 288)
+    dma("outd", T.y[:], v[6], [v], [])
+    for sem in SEMAPHORES:
+        if known["G"].get(sem, 0) < total[sem]:
+            g.wait_ge(T.sem[sem], total[sem])

@@ -11,10 +11,10 @@ MASKS = [1, 2, 3]
 
 SCRATCH = {}
 for _t, _s in (
-        ("float32", "pf 8 it0 320 it1 320 it2 320 neg8 8 own8 8 offadd 144 offt 144 offe 144 offo 144 msel 144 mselt 144 cvf 288 ssb 288 sr 2304 dm 288 d1 144 d2 72 d3 36 sc 24 r17 18 qf 18 pof 18 sort 288 spm 16 spv 4 sp8 16 wm 272 wn 72 wt 72 off32 144 off33 144 ntf 32 ntt 32 en 504 rt 1152 ysb 288"),
-        ("int32", "pi 8 ii 256 wli 64 rr 18 q32 18 nt 32 ph 96"),
+        ("float32", "pf 8 gm 8 it0 320 it1 320 it2 320 neg8 8 own8 8 offadd 144 offt 144 offe 144 offo 144 msel 144 mselt 144 cvf 288 bigm 288 ssb 288 sst 288 sr 2304 dm 288 d1 144 d2 72 d3 36 sc 24 rs 18 r17 18 qf 18 pof 18 sort 288 spm 16 spv 4 sp8 24 wm 272 wn 72 wt 72 off32 144 off33 144 ntf 32 ntt 32 en 504 rt 1152"),
+        ("int32", "pi 8 ii 256 rr 18 q32 18 nt 32 ph 96"),
         ("uint16", "clist 18 ul 72 wl 64 posl 18 off 144 phl 18 tl 72 hl 72"),
-        ("bfloat16", "gm 8 mk16 288 mk17 288 tri 288 mk272 272 cval 288 ones 64 zer 2304 ef 4096 ob 512 zb 1024 zz 1792 xt 1152 ut 512 vt 512 et 288 ml 5760 mc 2304 mf 2304 iw0 2304 iw1 2304 iw2 2304 itr 2304 fw 2304 ow 1152 tt 1152 o2 1152 tw 2304"),
+        ("bfloat16", "dump 1152 mk16 288 mk17 288 mk272 272 cval 288 ones 64 zer 2304 ef 4096 ob 512 zb 1024 zz 1792 xt 1152 ut 512 vt 512 ml 5760 mc 2304 mf 2304 iw0 2304 iw1 2304 iw2 2304 itr 2304 fw 2304 ow 1152 tt 1152 o2 1152 tw 2304"),
         ("mx", "ef 1024 ob 128 zb 256 zz 448 u 128 v 128 up 1152 w 512 wl 1024 x 288 ml 1440 mc 576 mf 576 tb 144 ta0 144 ta1 144 ta2 144 lc0 144 lc1 144 lc2 144")):
     _s = _s.split()
     for _n, _w in zip(_s[::2], _s[1::2]):
@@ -26,7 +26,7 @@ for _t, _s in (
 for _m in range(8):
     SCRATCH["p%d" % _m] = ("psum", [128, 512], "float32")
 
-SEMAPHORES = "sv sa st sg lx lu lw ls lv z0 z1 z2 z3 z4 outd arr0 arr1 arr2 sent0 sent1 sent2".split()
+SEMAPHORES = "sv sa st sg lx lu lw ls lv z0 z1 z2 z3 z4 z5 z6 outd arr0 arr1 arr2 sent0 sent1 sent2".split()
 
 
 def rank_program(g, core, T, topo):
@@ -60,7 +60,7 @@ def rank_program(g, core, T, topo):
                 bank = SCRATCH[v[0]][0] == "psum"
                 for (k2, q2, v2, sem, val) in hist.get(v[0], []):
                     if q2 == q and q in "VSTG":
-                        if k2 == "r" or (group and bank) or not clash(v, v2):
+                        if (kind == "r" and k2 == "r") or (group and bank) or not clash(v, v2):
                             continue
                     elif not bank and ((kind == "r" and k2 == "r") or not clash(v, v2)):
                         continue
@@ -119,8 +119,14 @@ def rank_program(g, core, T, topo):
     def fill(out, c):
         run("V", lambda: g.vector.memset(out[6], c), [], [out])
 
-    def gather(out, win, off):
-        run("V", lambda: g.vector.tensor_copy(out[6], win[6].indirect(off[6])), [win, off], [out])
+    def fetch(out, win, off):
+        run("S", lambda: g.scalar.activation(out[6], win[6].indirect(off[6]), ACT.Copy), [win, off], [out])
+
+    def gather2(out, c0, win, off, o0, n):
+        m = n // 2
+        a, e = view(out, c0, c0 + 16 * m), view(off, o0, o0 + m)
+        run("V", lambda: g.vector.tensor_copy(a[6], win[6].indirect(e[6])), [win, e], [a])
+        fetch(view(out, c0 + 16 * m, c0 + 16 * n), win, view(off, o0 + m, o0 + n))
 
     def fused(out, win, off, b, op):
         run("V", lambda: g.vector.tensor_tensor(out[6], win[6].indirect(off[6]), b[6], op), [win, off, b], [out])
@@ -136,7 +142,9 @@ def rank_program(g, core, T, topo):
         run("V", lambda: g.vector.quantize_mx(o[6], p[6], a[6]), [a], [o, p])
 
     def act(out, a, f=ACT.Copy, scale=1.0):
-        if scale == 1.0:
+        if isinstance(scale, tuple):
+            run("S", lambda: g.scalar.activation(out[6], a[6], f, scale=scale[6]), [a, scale], [out])
+        elif scale == 1.0:
             run("S", lambda: g.scalar.activation(out[6], a[6], f), [a], [out])
         else:
             run("S", lambda: g.scalar.activation(out[6], a[6], f, scale=scale), [a], [out])
@@ -158,7 +166,7 @@ def rank_program(g, core, T, topo):
     def pick(dst, src, n0, n1, w, off):
         o, i, o2, i2 = view(dst + "_q", n0, n1), view(src + "_q", 0, w), view(dst + "_s", n0, n1), view(src + "_s", 0, w)
         run("V", lambda: g.vector.tensor_copy(o[6].bitcast(dt.uint32), i[6].bitcast(dt.uint32).indirect(off[6])), [i, off], [o])
-        run("S", lambda: g.scalar.activation(o2[6], i2[6].indirect(off[6]), ACT.Copy), [i2, off], [o2])
+        fetch(o2, i2, off)
 
     for sem, name, src, w in (("lx", "xt", T.x, 1152), ("lu", "ut", T.u, 512)):
         dma(sem, T[name][:, 0:w], src[:], [], [view(name, 0, w)])
@@ -180,7 +188,7 @@ def rank_program(g, core, T, topo):
     iota(view("ii", 96, 160), [[16, 8], [128, 4], [0, 2]], f=False)
 
     fill(view("zer", 0, 2304), 0.0)
-    for sem, name, c0, c1 in (("z0", "ef", 0, 2304), ("z1", "ef", 2304, 4096), ("z2", "iw0", 0, 2304), ("z3", "iw1", 0, 2304), ("z4", "iw2", 0, 2304)):
+    for sem, name, c0, c1 in (("z0", "ef", 0, 2304), ("z1", "ef", 2304, 4096), ("z5", "zb", 0, 1024), ("z6", "zz", 0, 1792), ("z2", "iw0", 0, 2304), ("z3", "iw1", 0, 2304), ("z4", "iw2", 0, 2304)):
         dma(sem, T[name][:, c0:c1], T.zer[:, 0:c1 - c0], [view("zer", 0, c1 - c0)], [view(name, c0, c1)])
     fill(view("ones", 0, 64), 1.0)
     ts(pi[1], pi[0], 15, OP.bitwise_and)
@@ -198,8 +206,15 @@ def rank_program(g, core, T, topo):
     ts(pcol[6], pi[6], 4096.0, OP.mult)
     ts(pcol[7], pi[6], -4096.0, OP.mult, 4096.0, OP.add)
     ts(view("mk16", 0, 288), view("it0", 0, 288), pcol[0], OP.is_equal)
+    ts(view("bigm", 0, 288), view("it0", 0, 288), pcol[0], OP.is_le, BIG, OP.mult)
+    ts(view("gm", 0, 8), view("it1", 144, 152), pcol[1], OP.is_equal)
     tc(view("clist", 0, 18), view("ii", 72, 90))
     fill(view("sc", 16, 24), 0.0)
+    fill(view("rs", 0, 1), 0.0)
+    fill(view("ml", 0, 512), 0.0)
+    fill(view("ml", 1152, 1664), 0.0)
+    for a, w in ((8, 176), (9, 176), (10, 176), (12, 240), (13, 240), (14, 240), (16, 288), (17, 288)):
+        fill(view("ml", 1152 * (a // 4) + 64 * a + a % 4, 1152 * (a // 4) + 4 * w, 4), 0.0)
     for h in range(8):
         for t in range(4):
             o, i = view("ef", 512 * h + 128 * t + t, 512 * h + 128 * t + 128, 4), view("ones", 0, 32)
@@ -209,15 +224,15 @@ def rank_program(g, core, T, topo):
 
     def constants_1():
         pick("up", "u", 128, 1152, 128, view("ul", 8, 72))
-        ts(view("gm", 0, 8), view("it1", 144, 152), pcol[1], OP.is_equal)
-        ts(view("tri", 0, 288), view("it0", 0, 288), pcol[0], OP.is_gt)
-        fill(view("ml", 4 * 1152 + 3, 5760, 4), 0.0)
         for k in range(8):
-            ts(view("ob", 64 * k, 64 * k + 64), view("ones", 0, 64), view("gm", k, k + 1), OP.mult)
+            act(view("ob", 64 * k, 64 * k + 64), view("ones", 0, 64), ACT.Copy, view("gm", k, k + 1))
         quant("ob", view("ob", 0, 512), 0, 128)
+        for z in range(4):
+            for b in range(4):
+                act(view("zb", 512 * (z // 2) + 16 * z + 5 * b, 512 * (z // 2) + 512, 64), view("gm", 0, 8))
 
     def constants_2():
-        ts(view("mk17", 0, 288), view("mk16", 0, 288), 17.0, OP.mult)
+        act(view("mk17", 0, 288), view("mk16", 0, 288), ACT.Copy, 17.0)
         ts(view("neg8", 0, 8), view("it1", 144, 152), pcol[1], OP.is_lt, -1.0, OP.mult)
         ts(view("own8", 0, 8), view("it1", 144, 152), pcol[1], OP.is_equal, -BIG, OP.mult)
         ts(view("offadd", 0, 144), view("it1", 0, 144), pcol[1], OP.is_lt, 24.0, OP.mult)
@@ -226,12 +241,6 @@ def rank_program(g, core, T, topo):
         ts(view("offe", 0, 144), view("offadd", 0, 144), pcol[6], OP.subtract)
         ts(view("offo", 0, 144), view("offadd", 0, 144), pcol[7], OP.subtract)
         ts(view("mk272", 0, 272), view("it2", 0, 272), pcol[0], OP.is_equal)
-        fill(view("zb", 0, 1024), 0.0)
-        for z in range(4):
-            for b in range(4):
-                tc(view("zb", 512 * (z // 2) + 16 * z + 5 * b, 512 * (z // 2) + 512, 64), view("gm", 0, 8))
-        quant("zb", view("zb", 0, 1024), 0, 256)
-        fill(view("zz", 0, 1792), 0.0)
         for w in range(2):
             for b in range(4):
                 fill(view("zz", 896 * w + 384 + 5 * b, 896 * w + 512, 16), 16.0 if w else 1.0)
@@ -245,15 +254,17 @@ def rank_program(g, core, T, topo):
         fill(view("cval", 144, 145), 0.25)
         quant("ef", view("ef", 0, 2048), 0, 512)
         quant("ef", view("ef", 2048, 4096), 512, 1024)
+        quant("zb", view("zb", 0, 1024), 0, 256)
 
     def constants_3():
-        ts(view("wli", 0, 64), view("ii", 96, 160), pcol[0], OP.add)
-        tc(view("wl", 0, 64), view("wli", 0, 64))
+        ts(view("ii", 160, 224), view("ii", 96, 160), pcol[0], OP.add)
+        tc(view("wl", 0, 64), view("ii", 160, 224))
         pick("wl", "w", 0, 1024, 512, view("wl", 0, 64))
         quant("v", view("vt", 0, 512), 0, 128)
 
-    def tree(v, out):
+    def tree(v, out, beside=lambda: None):
         tt(view("d1", 0, 144), view(v, 0, 288, 2), view(v, 1, 288, 2), OP.add)
+        beside()
         tt(view("d2", 0, 72), view("d1", 0, 144, 2), view("d1", 1, 144, 2), OP.add)
         tt(view("d3", 0, 36), view("d2", 0, 72, 2), view("d2", 1, 72, 2), OP.add)
         tt(out, view("d3", 0, 36, 2), view("d3", 1, 36, 2), OP.add)
@@ -262,30 +273,44 @@ def rank_program(g, core, T, topo):
         mm(0, C, "up", 0, "x", 0)
         tt(view("dm", 0, 288), ps(0, 0, 288), view("mk16", 0, 288), OP.mult)
         tc(view("ssb", 0, 288), ps(0, 0, 288))
-        tree("dm", view("sc", 0, 18))
+        tree("dm", view("sc", 0, 18), lambda: tt(view("sst", 0, 288), ps(0, 0, 288), view("bigm", 0, 288), OP.add))
         if rnd == 0:
             constants_1()
-        for k in range(8):
+
+        def sr_rows(ks):
+            for k in ks:
+                act(view("sr", 288 * k, 288 * k + 288), ps(2 + k % 4, 0, 288))
+
+        for k in range(4):
             mm(2 + k % 4, C, "up", 128 + 128 * k, "x", 0)
-            act(view("sr", 288 * k, 288 * k + 288), ps(2 + k % 4, 0, 288))
-        fused(view("et", 0, 288), view("sc", 0, 24), view("clist", 0, 18), view("ssb", 0, 288), OP.is_equal)
-        tt(view("ml", 4 * 1152 + 2, 5760, 4), view("et", 0, 288), view("tri", 0, 288), OP.mult)
-        for al in range(5):
-            for a in range(4 * al, min(18, 4 * al + 4)):
-                c = 16 * a + 16
-                ts(view("ml", 1152 * al + a % 4, 1152 * al + 4 * c, 4), view("ssb", 0, c), view("sc", a, a + 1), OP.is_lt)
-                if c < C:
-                    ts(view("ml", 1152 * al + 4 * c + a % 4, 1152 * al + 1152, 4), view("ssb", c, C), view("sc", a, a + 1), OP.is_le)
-            quant("ml", view("ml", 1152 * al, 1152 * al + 1152), 288 * al, 288 * al + 288)
-            mm(1, C, "ob", 0, "ml", 288 * al, al == 0, al == 4)
+        sr_rows(range(4))
+        for k in range(4, 8):
+            mm(2 + k % 4, C, "up", 128 + 128 * k, "x", 0)
+        for al in (4, 3, 2, 1, 0):
+            w = C if al == 4 else max(128, 64 * al + 48)
+            aa = [a for a in range(4 * al, min(18, 4 * al + 4)) if a]
+            for a in aa:
+                ts(view("ml", 1152 * al + a % 4, 1152 * al + 64 * a, 4), view("ssb", 0, 16 * a), view("sc", a, a + 1), OP.is_lt)
+            if al == 4:
+                fused(view("ml", 4 * 1152 + 2, 5760, 4), view("sc", 0, 24), view("clist", 0, 18), view("sst", 0, 288), OP.is_equal)
+                fused(view("ml", 4 * 1152 + 3, 5760, 4), view("sc", 0, 24), view("clist", 0, 18), view("ssb", 0, 288), OP.is_gt)
+            quant("ml", view("ml", 1152 * al, 1152 * al + 4 * w), 288 * al, 288 * al + w)
+            mm(1, w, "ob", 0, "ml", 288 * al, al == 4, al == 0)
+            for a in aa:
+                i, o, acc = view("ml", 1152 * al + a % 4, 1152 * al + 64 * a, 4), view("dump", 288 * (a % 4), 288 * (a % 4) + 16 * a), view("rs", a, a + 1)
+                run("S", lambda: g.scalar.activation(o[6], i[6], ACT.Identity, bias=17.0, scale=-17.0, accum_out=acc[6]), [i], [o, acc])
+        sr_rows(range(4, 8))
         if rnd == 0:
             constants_2()
         for k in range(8):
             mm(2 + k % 4, C, "ef", 128 * k, "x", 0)
             act(view("fw", 288 * k, 288 * k + 288), ps(2 + k % 4, 0, 288))
+        for k, gr in enumerate((2, 3, 6, 7)):
+            mm(2 + k, C, "up", 128 + 128 * gr, "x", 0)
         tt(view("dm", 0, 288), ps(1, 0, 288), view("mk17", 0, 288), OP.mult)
         r17 = view("r17", 0, 18)
         tree("dm", r17)
+        tt(r17, r17, view("rs", 0, 18), OP.add)
         ts(view("q32", 0, 18), r17, 1.0 / 289.0, OP.mult, -136.0 / 289.0, OP.add)
         ts(view("qf", 0, 18), view("q32", 0, 18), -288.0, OP.mult)
         tt(view("pof", 0, 18), r17, view("qf", 0, 18), OP.add)
@@ -294,29 +319,38 @@ def rank_program(g, core, T, topo):
         sm = view("spm", 0, 16)
         tt(sm, view("sort", 272, 288), view("mk16", 0, 16), OP.mult)
         sp, spa, dec = view("spv", 0, 1), view("spv", 1, 2), view("spv", 2, 3)
-        run("V", lambda: g.vector.tensor_reduce(sp[6], sm[6], AxisListType.X, OP.add), [sm], [sp])
         run("V", lambda: g.vector.tensor_reduce(spa[6], sm[6], AxisListType.X, OP.add, apply_absolute_value=True), [sm], [spa])
+        run("V", lambda: g.vector.tensor_reduce(sp[6], sm[6], AxisListType.X, OP.add), [sm], [sp])
         ts(dec, spa, EPS, OP.mult, DELTA, OP.add)
         ts(view("sp8", 0, 8), view("neg8", 0, 8), dec, OP.mult, sp, OP.add)
         tt(view("sp8", 8, 16), view("sp8", 0, 8), view("own8", 0, 8), OP.add)
-        for hf in range(2):
-            for gr in range(4 * hf, 4 * hf + 4):
-                ts(view("mc", 288 * gr, 288 * gr + 288), view("sr", 288 * gr, 288 * gr + 288), view("sp8", 8 + gr, 9 + gr), OP.is_le)
-            quant("mc", view("mc", 1152 * hf, 1152 * hf + 1152), 288 * hf, 288 * hf + 288)
-            for z in range(2):
-                mm(6 + hf, 286, "zb", 128 * z, "mc", 288 * hf + 2 * z, z == 0, z == 1)
+        ts(view("sp8", 16, 24), view("sp8", 8, 16), dec, OP.add)
+        runs = [lambda: tt(view("wm", 0, 272), view("sort", 0, 272), view("mk272", 0, 272), OP.mult),
+                lambda: tt(view("wm", 0, 136), view("wm", 0, 136), view("wm", 136, 272), OP.add),
+                lambda: tt(view("wm", 0, 68), view("wm", 0, 68), view("wm", 68, 136), OP.add),
+                lambda: tt(view("wm", 0, 34), view("wm", 0, 34), view("wm", 34, 68), OP.add),
+                lambda: tt(view("wn", 0, 17), view("wm", 0, 17), view("wm", 17, 34), OP.add),
+                lambda: [ts(view("wt", 0, 17), view("wn", 0, 17), EPS, OP.mult, -DELTA, OP.add),
+                         ts(view("wt", 24, 41), view("wn", 0, 17), -EPS, OP.mult, -DELTA, OP.add)],
+                lambda: tt(view("wt", 48, 65), view("wt", 0, 17), view("wt", 24, 41), OP.min),
+                lambda: [tt(view("wn", 24, 41), view("wn", 0, 17), view("wt", 48, 65), OP.add), ts(view("rr", 0, 18), r17, 1.0 / 17.0, OP.mult)]]
+        for gr in range(8):
+            o, i = view("mc", 288 * gr, 288 * gr + 288), view("sr", 288 * gr, 288 * gr + 288)
+            if gr % 4 >= 2:
+                s, b = view("dump", 288 * (gr % 4), 288 * (gr % 4) + 288), view("sp8", 16 + gr, 17 + gr)
+                run("S", lambda: g.scalar.activation(s[6], i[6], ACT.Sign, bias=b[6], scale=-1.0), [i, b], [s])
+                act(o, s, ACT.Relu)
+            else:
+                ts(o, i, view("sp8", 8 + gr, 9 + gr), OP.is_le)
+            runs[gr]()
+            if gr % 4 == 3:
+                hf = gr // 4
+                quant("mc", view("mc", 1152 * hf, 1152 * hf + 1152), 288 * hf, 288 * hf + 288)
+                for z in range(2):
+                    mm(6 + hf, 286, "zb", 128 * z, "mc", 288 * hf + 2 * z, z == 0, z == 1)
         for k in range(4):
             for w in range(2):
                 mm(1, H, "zz", 224 * w + 96 - 32 * k, "mc", 144 * k, k == 0 and w == 0, False)
-        tt(view("wm", 0, 272), view("sort", 0, 272), view("mk272", 0, 272), OP.mult)
-        for n in (136, 68, 34):
-            tt(view("wm", 0, n), view("wm", 0, n), view("wm", n, 2 * n), OP.add)
-        tt(view("wn", 0, 17), view("wm", 0, 17), view("wm", 17, 34), OP.add)
-        ts(view("wt", 0, 17), view("wn", 0, 17), EPS, OP.mult, -DELTA, OP.add)
-        ts(view("wt", 24, 41), view("wn", 0, 17), -EPS, OP.mult, -DELTA, OP.add)
-        tt(view("wt", 48, 65), view("wt", 0, 17), view("wt", 24, 41), OP.min)
-        tt(view("wn", 24, 41), view("wn", 0, 17), view("wt", 48, 65), OP.add)
-        ts(view("rr", 0, 18), r17, 1.0 / 17.0, OP.mult)
         for hf in range(2):
             c0, c1 = 72 * hf, 72 * hf + 72
             o, o2 = view("off32", c0, c1), view("off33", c0, c1)
@@ -324,11 +358,18 @@ def rank_program(g, core, T, topo):
             tt(o2, ps(6 + hf, 1, 286, 4), view("offo", c0, c1), OP.add)
             tt(o, o, o2, OP.max)
             tc(view("off", c0, c1), o)
-        for k in range(4):
-            o = view("mf", 576 * k, 576 * k + 576)
-            fused(o, view("wn", 0, 72), view("off", 36 * k, 36 * k + 36), view("sr", 576 * k, 576 * k + 576), OP.is_ge)
-            quant("mf", o, 144 * k, 144 * k + 144)
-            mm(1, H, "zz", 96 - 32 * k, "mf", 144 * k, False, k == 3)
+            w = view("wn", 0, 72)
+            fetch(view("rt", 576 * hf, 576 * hf + 576), w, view("off", c0 + 36, c1))
+            for k in (2 * hf, 2 * hf + 1):
+                m = view("mf", 576 * k, 576 * k + 576)
+                if k % 2 == 0:
+                    fused(m, w, view("off", 36 * k, 36 * k + 36), view("sr", 576 * k, 576 * k + 576), OP.is_ge)
+                else:
+                    for e in range(2):
+                        c = 576 * hf + 288 * e
+                        tt(view("mf", 576 * k + 288 * e, 576 * k + 288 * e + 288), view("rt", c, c + 288), ps(2 + 2 * hf + e, 0, 288), OP.is_ge)
+                quant("mf", m, 144 * k, 144 * k + 144)
+                mm(1, H, "zz", 96 - 32 * k, "mf", 144 * k, False, k == 3)
         tt(view("wm", 0, 144), ps(1, 0, 144), view("mselt", 0, 144), OP.mult)
         tt(view("d2", 0, 72), view("wm", 0, 72), view("wm", 72, 144), OP.add)
         tt(view("d3", 0, 36), view("d2", 0, 72, 2), view("d2", 1, 72, 2), OP.add)
@@ -390,7 +431,7 @@ def rank_program(g, core, T, topo):
         places(rnd)
         seats(rnd)
         ta, lc = "ta%d" % rnd, "lc%d" % rnd
-        gather(view("ow", 0, 576), view("fw", 0, 2304), view("tl", 0, 36))
+        gather2("ow", 0, view("fw", 0, 2304), "tl", 0, 36)
         native("tt", 0, "ow", 0, 144, 4, ALL)
         quant(ta, view("tt", 0, 576), 0, 144)
         dst = T.cores[rank ^ MASKS[rnd]]
@@ -402,7 +443,7 @@ def rank_program(g, core, T, topo):
         g.remote_dma(T[lc + "_s"][:, 0:144], T[ta + "_s"][:, 0:144], T.sem[arr], T.sem[sent], pid, rid, mask)
         total[arr] = total[sent] = 2 * ne
         note("R", arr, 2 * ne, [], [view(lc + "_q", 0, 144), view(lc + "_s", 0, 144)])
-        gather(view("ow", 576, 1152), view("fw", 0, 2304), view("tl", 36, 72))
+        gather2("ow", 576, view("fw", 0, 2304), "tl", 36, 36)
         native("tt", 576, "ow", 576, 144, 4, ALL)
         quant("tb", view("tt", 576, 1152), 0, 144)
         if rnd == 0:
@@ -421,7 +462,7 @@ def rank_program(g, core, T, topo):
                 dma("outd", T.pl[gr:gr + 1, :], v[6], [v], [])
         layer(lc, 0)
         for k in range(2):
-            gather(view("o2", 576 * k, 576 * k + 576), view("tw", 0, 2304), view("hl", 36 * k, 36 * k + 36))
+            gather2("o2", 576 * k, view("tw", 0, 2304), "hl", 36 * k, 36)
             native("xt", 0, "o2", 0, 288, 1, ALL[8 * k:8 * k + 8])
     quant("x", view("xt", 0, 1152), 0, 288)
     mm(0, C, "v", 0, "x", 0)
@@ -430,8 +471,8 @@ def rank_program(g, core, T, topo):
     for k in range(4):
         v = view("x_s", 0, 288, 1, 32 * k, 32 * k + 4)
         dma("outd", T.osc[4 * k:4 * k + 4, :], v[6], [v], [])
-    tc(view("ysb", 0, 288), ps(0, 0, 288))
-    v = view("ysb", 0, 288)
+    tc(view("dm", 0, 288), ps(0, 0, 288))
+    v = view("dm", 0, 288)
     dma("outd", T.y[:], v[6], [v], [])
     for sem in SEMAPHORES:
         if known["G"].get(sem, 0) < total[sem]:

@@ -11,10 +11,10 @@ MASKS = [1, 2, 3]
 
 SCRATCH = {}
 for _t, _s in (
-        ("float32", "pf 8 gm 8 it0 320 it1 320 it2 320 neg8 8 own8 8 offadd 144 offt 144 offe 144 offo 144 msel 144 mselt 144 cvf 288 bigm 288 ssb 288 sst 288 sr 2304 dm 288 d1 144 d2 72 d3 36 sc 24 rs 18 r17 18 qf 18 pof 18 sort 288 spm 16 spv 4 sp8 24 wm 272 wn 72 wt 72 off32 144 off33 144 ntf 32 ntt 32 en 504 rt 1152"),
-        ("int32", "pi 8 ii 256 rr 18 q32 18 nt 32 ph 96"),
+        ("float32", "pf 16 gm 8 it0 320 it1 320 it2 320 neg8 8 own8 8 offadd 144 offt 144 offe 144 offo 144 msel 144 mselt 144 cvf 288 bigm 288 ssb 288 sst 288 sr 2304 dm 288 sc 288 rs 18 rk 18 pof 18 nc 144 sort 288 spm 16 spv 4 sp8 24 wm 288 wr 288 wn 72 wt 72 off32 144 off33 144 ntf 32 ntt 32 en 504 rt 1152"),
+        ("int32", "pi 8 ii 256 nt 32 ph 96"),
         ("uint16", "clist 18 ul 72 wl 64 posl 18 off 144 phl 18 tl 72 hl 72"),
-        ("bfloat16", "dump 1152 mk16 288 mk17 288 mk272 272 cval 288 ones 64 zer 2304 ef 4096 ob 512 zb 1024 zz 1792 xt 1152 ut 512 vt 512 ml 5760 mc 2304 mf 2304 iw0 2304 iw1 2304 iw2 2304 itr 2304 fw 2304 ow 1152 tt 1152 o2 1152 tw 2304"),
+        ("bfloat16", "dump 1152 mk16 288 mk17 288 kp16 288 kp17 288 kp4 144 cval 288 ones 64 zer 2304 ef 4096 ob 512 zb 1024 zz 1792 xt 1152 ut 512 vt 512 ml 5760 mc 2304 mf 2304 iw0 2304 iw1 2304 iw2 2304 itr 2304 fw 2304 ow 1152 tt 1152 o2 1152 tw 2304"),
         ("mx", "ef 1024 ob 128 zb 256 zz 448 u 128 v 128 up 1152 w 512 wl 1024 x 288 ml 1440 mc 576 mf 576 tb 144 ta0 144 ta1 144 ta2 144 lc0 144 lc1 144 lc2 144")):
     _s = _s.split()
     for _n, _w in zip(_s[::2], _s[1::2]):
@@ -119,6 +119,9 @@ def rank_program(g, core, T, topo):
     def fill(out, c):
         run("V", lambda: g.vector.memset(out[6], c), [], [out])
 
+    def sums(out, keep, a):
+        run("V", lambda: g.vector.tensor_tensor_scan(out[6], keep[6], a[6], 0.0, OP.mult, OP.add), [keep, a], [out])
+
     def fetch(out, win, off):
         run("S", lambda: g.scalar.activation(out[6], win[6].indirect(off[6]), ACT.Copy), [win, off], [out])
 
@@ -141,9 +144,11 @@ def rank_program(g, core, T, topo):
         o, p = view(n + "_q", c0, c1), view(n + "_s", c0, c1)
         run("V", lambda: g.vector.quantize_mx(o[6], p[6], a[6]), [a], [o, p])
 
-    def act(out, a, f=ACT.Copy, scale=1.0):
+    def act(out, a, f=ACT.Copy, scale=1.0, bias=0.0):
         if isinstance(scale, tuple):
             run("S", lambda: g.scalar.activation(out[6], a[6], f, scale=scale[6]), [a, scale], [out])
+        elif bias:
+            run("S", lambda: g.scalar.activation(out[6], a[6], ACT.Identity, bias=bias, scale=scale), [a], [out])
         elif scale == 1.0:
             run("S", lambda: g.scalar.activation(out[6], a[6], f), [a], [out])
         else:
@@ -173,16 +178,17 @@ def rank_program(g, core, T, topo):
     dma("lw", T.w_q[:, 0:512].bitcast(dt.uint8), T.wc[:], [], [view("w_q", 0, 512)])
     dma("ls", T.w_s[:, 0:512], T.ws[:], [], [view("w_s", 0, 512)])
     dma("lv", T.vt[:, 0:512], T.v[:], [], [view("vt", 0, 512)])
-    pcol = [view("pf", k, k + 1) for k in range(8)]
+    pf = [view("pf", k, k + 1) for k in range(11)]
+    kappa, group, parity, kap4 = pf[1], pf[2], pf[3], pf[5]
     pi = [view("pi", k, k + 1) for k in range(8)]
     iota(pi[0], [[0, 1]], 0, 1, f=False)
     iota(view("ii", 0, 8), [[16, 8]], f=False)
     iota(view("ii", 8, 72), [[16, 8], [0, 8]], f=False)
     iota(view("it0", 0, 288), [[0, 18], [1, 16]])
     iota(view("it1", 144, 152), [[1, 8]])
-    iota(view("ii", 72, 90), [[1, 18]], f=False)
+    iota(view("ii", 72, 90), [[16, 18]], 15, 0, f=False)
     iota(view("it1", 0, 144), [[1, 8], [0, 18]])
-    iota(view("it2", 0, 272), [[1, 16], [0, 17]])
+    iota(view("it2", 0, 289), [[0, 17], [1, 17]])
     iota(view("cvf", 0, 288), [[1, 288]], -144, 0)
     iota(view("it1", 160, 304), [[0, 36], [1, 4]])
     iota(view("ii", 96, 160), [[16, 8], [128, 4], [0, 2]], f=False)
@@ -191,36 +197,36 @@ def rank_program(g, core, T, topo):
     for sem, name, c0, c1 in (("z0", "ef", 0, 2304), ("z1", "ef", 2304, 4096), ("z5", "zb", 0, 1024), ("z6", "zz", 0, 1792), ("z2", "iw0", 0, 2304), ("z3", "iw1", 0, 2304), ("z4", "iw2", 0, 2304)):
         dma(sem, T[name][:, c0:c1], T.zer[:, 0:c1 - c0], [view("zer", 0, c1 - c0)], [view(name, c0, c1)])
     fill(view("ones", 0, 64), 1.0)
+    fill(view("rs", 0, 1), 0.0)
+    act(view("ml", 0, 512), view("zer", 0, 512))
+    act(view("ml", 1152, 1664), view("zer", 0, 512))
+    for al, b, c, w in ((2, 0, 144, 192), (2, 1, 160, 192), (2, 2, 176, 192), (3, 0, 208, 256), (3, 1, 224, 256), (3, 2, 240, 256), (4, 0, 272, 288), (4, 3, 0, 288)):
+        act(view("ml", 1152 * al + 4 * c + b, 1152 * al + 4 * w, 4), view("zer", 0, w - c))
+    tc(view("ul", 0, 72), view("ii", 0, 72))
     ts(pi[1], pi[0], 15, OP.bitwise_and)
     ts(pi[2], pi[0], 4, OP.logical_shift_right)
     ts(pi[3], pi[0], 4, OP.logical_shift_right, 1, OP.bitwise_and)
     ts(pi[4], pi[0], 5, OP.logical_shift_right)
     ts(pi[5], pi[0], 15, OP.bitwise_and, 2, OP.logical_shift_right)
-    tc(view("ul", 0, 72), view("ii", 0, 72))
-    for k in range(3):
-        tc(pcol[k], pi[k + 1])
-    ts(pcol[3], pi[4], 576, OP.mult, 144, OP.add)
-    ts(pcol[4], pi[4], 576, OP.mult, 432, OP.add)
-    tc(pcol[5], pi[5])
-    ts(pi[6], pi[5], 1, OP.bitwise_and)
-    ts(pcol[6], pi[6], 4096.0, OP.mult)
-    ts(pcol[7], pi[6], -4096.0, OP.mult, 4096.0, OP.add)
-    ts(view("mk16", 0, 288), view("it0", 0, 288), pcol[0], OP.is_equal)
-    ts(view("bigm", 0, 288), view("it0", 0, 288), pcol[0], OP.is_le, BIG, OP.mult)
-    ts(view("gm", 0, 8), view("it1", 144, 152), pcol[1], OP.is_equal)
-    tc(view("clist", 0, 18), view("ii", 72, 90))
-    fill(view("sc", 16, 24), 0.0)
-    fill(view("rs", 0, 1), 0.0)
-    fill(view("ml", 0, 512), 0.0)
-    fill(view("ml", 1152, 1664), 0.0)
-    for a, w in ((8, 176), (9, 176), (10, 176), (12, 240), (13, 240), (14, 240), (16, 288), (17, 288)):
-        fill(view("ml", 1152 * (a // 4) + 64 * a + a % 4, 1152 * (a // 4) + 4 * w, 4), 0.0)
+    ts(pi[6], pi[0], 4, OP.bitwise_and, 2, OP.logical_shift_right)
+    tc(view("pf", 0, 7), view("pi", 0, 7))
+    act(pf[7], pf[4], ACT.Identity, 576.0, 144.0)
+    act(pf[8], pf[4], ACT.Identity, 576.0, 432.0)
+    act(pf[9], pf[6], ACT.Copy, 4096.0)
+    act(pf[10], pf[6], ACT.Identity, -4096.0, 4096.0)
+    ts(view("mk16", 0, 288), view("it0", 0, 288), kappa, OP.is_equal)
+    ts(view("kp16", 0, 288), view("it0", 0, 288), 0.0, OP.not_equal)
+    ts(view("gm", 0, 8), view("it1", 144, 152), group, OP.is_equal)
     for h in range(8):
         for t in range(4):
             o, i = view("ef", 512 * h + 128 * t + t, 512 * h + 128 * t + 128, 4), view("ones", 0, 32)
             run("G", lambda: g.affine_select(o[6], i[6], [[0, 2], [-1, 16]], OP.is_equal, 0.0, -16 * h, 1), [i], [o])
     quant("u", view("ut", 0, 512), 0, 128)
     pick("up", "u", 0, 128, 128, view("ul", 0, 8))
+
+    def constants_0():
+        ts(view("bigm", 0, 288), view("it0", 0, 288), kappa, OP.is_le, BIG, OP.mult)
+        tc(view("clist", 0, 18), view("ii", 72, 90))
 
     def constants_1():
         pick("up", "u", 128, 1152, 128, view("ul", 8, 72))
@@ -232,48 +238,45 @@ def rank_program(g, core, T, topo):
                 act(view("zb", 512 * (z // 2) + 16 * z + 5 * b, 512 * (z // 2) + 512, 64), view("gm", 0, 8))
 
     def constants_2():
-        act(view("mk17", 0, 288), view("mk16", 0, 288), ACT.Copy, 17.0)
-        ts(view("neg8", 0, 8), view("it1", 144, 152), pcol[1], OP.is_lt, -1.0, OP.mult)
-        ts(view("own8", 0, 8), view("it1", 144, 152), pcol[1], OP.is_equal, -BIG, OP.mult)
-        ts(view("offadd", 0, 144), view("it1", 0, 144), pcol[1], OP.is_lt, 24.0, OP.mult)
-        ts(view("offt", 0, 144), view("it1", 0, 144), pcol[1], OP.is_equal, 48.0, OP.mult)
-        tt(view("offadd", 0, 144), view("offadd", 0, 144), view("offt", 0, 144), OP.add)
-        ts(view("offe", 0, 144), view("offadd", 0, 144), pcol[6], OP.subtract)
-        ts(view("offo", 0, 144), view("offadd", 0, 144), pcol[7], OP.subtract)
-        ts(view("mk272", 0, 272), view("it2", 0, 272), pcol[0], OP.is_equal)
         for w in range(2):
             for b in range(4):
-                fill(view("zz", 896 * w + 384 + 5 * b, 896 * w + 512, 16), 16.0 if w else 1.0)
-        quant("zz", view("zz", 0, 1792), 0, 448)
+                act(view("zz", 896 * w + 384 + 5 * b, 896 * w + 512, 16), view("ones", 0, 8), ACT.Copy, 16.0 if w else 1.0)
+        act(view("cval", 0, 288), view("cvf", 0, 288))
+        ts(view("neg8", 0, 8), view("it1", 144, 152), group, OP.is_lt, -1.0, OP.mult)
+        ts(view("own8", 0, 8), view("it1", 144, 152), group, OP.is_equal, -BIG, OP.mult)
+        ts(view("offadd", 0, 144), view("it1", 0, 144), group, OP.is_lt, 24.0, OP.mult)
+        ts(view("offt", 0, 144), view("it1", 0, 144), group, OP.is_equal, 48.0, OP.mult)
+        ts(view("kp17", 0, 288), view("it2", 0, 288), 0.0, OP.not_equal)
+        tt(view("offadd", 0, 144), view("offadd", 0, 144), view("offt", 0, 144), OP.add)
+        ts(view("kp4", 0, 144), view("it1", 160, 304), 0.0, OP.not_equal)
+        ts(view("offe", 0, 144), view("offadd", 0, 144), pf[9], OP.subtract)
+        ts(view("offo", 0, 144), view("offadd", 0, 144), pf[10], OP.subtract)
+        ts(view("mk17", 0, 288), view("it2", 0, 288), kappa, OP.is_equal)
         fill(view("wn", 0, 48), 0.0)
         fill(view("wn", 48, 72), -BIG)
-        ts(view("msel", 0, 144), view("it1", 160, 304), pcol[5], OP.is_equal)
-        ts(view("mselt", 0, 144), view("msel", 0, 144), pcol[2], OP.mult)
-        tt(view("mselt", 0, 72), view("msel", 0, 72), view("mselt", 0, 72), OP.subtract)
-        tc(view("cval", 0, 288), view("cvf", 0, 288))
-        fill(view("cval", 144, 145), 0.25)
+        ts(view("msel", 0, 144), view("it1", 160, 304), kap4, OP.is_equal)
+        ts(view("mselt", 0, 144), view("msel", 0, 144), parity, OP.mult)
         quant("ef", view("ef", 0, 2048), 0, 512)
+        tt(view("mselt", 0, 72), view("msel", 0, 72), view("mselt", 0, 72), OP.subtract)
         quant("ef", view("ef", 2048, 4096), 512, 1024)
         quant("zb", view("zb", 0, 1024), 0, 256)
+        quant("zz", view("zz", 0, 1792), 0, 448)
+        fill(view("cval", 144, 145), 0.25)
 
     def constants_3():
-        ts(view("ii", 160, 224), view("ii", 96, 160), pcol[0], OP.add)
+        ts(view("ii", 160, 224), view("ii", 96, 160), kappa, OP.add)
         tc(view("wl", 0, 64), view("ii", 160, 224))
         pick("wl", "w", 0, 1024, 512, view("wl", 0, 64))
         quant("v", view("vt", 0, 512), 0, 128)
 
-    def tree(v, out, beside=lambda: None):
-        tt(view("d1", 0, 144), view(v, 0, 288, 2), view(v, 1, 288, 2), OP.add)
-        beside()
-        tt(view("d2", 0, 72), view("d1", 0, 144, 2), view("d1", 1, 144, 2), OP.add)
-        tt(view("d3", 0, 36), view("d2", 0, 72, 2), view("d2", 1, 72, 2), OP.add)
-        tt(out, view("d3", 0, 36, 2), view("d3", 1, 36, 2), OP.add)
-
     def places(rnd):
         mm(0, C, "up", 0, "x", 0)
+        if rnd == 0:
+            constants_0()
         tt(view("dm", 0, 288), ps(0, 0, 288), view("mk16", 0, 288), OP.mult)
         tc(view("ssb", 0, 288), ps(0, 0, 288))
-        tree("dm", view("sc", 0, 18), lambda: tt(view("sst", 0, 288), ps(0, 0, 288), view("bigm", 0, 288), OP.add))
+        sums(view("sc", 0, 288), view("kp16", 0, 288), view("dm", 0, 288))
+        tt(view("sst", 0, 288), ps(0, 0, 288), view("bigm", 0, 288), OP.add)
         if rnd == 0:
             constants_1()
 
@@ -287,18 +290,18 @@ def rank_program(g, core, T, topo):
         for k in range(4, 8):
             mm(2 + k % 4, C, "up", 128 + 128 * k, "x", 0)
         for al in (4, 3, 2, 1, 0):
-            w = C if al == 4 else max(128, 64 * al + 48)
-            aa = [a for a in range(4 * al, min(18, 4 * al + 4)) if a]
+            w = C if al == 4 else max(128, 64 * al + 64)
+            aa = range(4 * al, min(18, 4 * al + 4))
             for a in aa:
-                ts(view("ml", 1152 * al + a % 4, 1152 * al + 64 * a, 4), view("ssb", 0, 16 * a), view("sc", a, a + 1), OP.is_lt)
+                ts(view("ml", 1152 * al + a % 4, 1152 * al + 64 * a + 64, 4), view("ssb", 0, 16 * a + 16), view("sc", 16 * a + 15, 16 * a + 16), OP.is_lt)
             if al == 4:
-                fused(view("ml", 4 * 1152 + 2, 5760, 4), view("sc", 0, 24), view("clist", 0, 18), view("sst", 0, 288), OP.is_equal)
-                fused(view("ml", 4 * 1152 + 3, 5760, 4), view("sc", 0, 24), view("clist", 0, 18), view("ssb", 0, 288), OP.is_gt)
+                fused(view("ml", 4 * 1152 + 2, 5760, 4), view("sc", 0, 288), view("clist", 0, 18), view("sst", 0, 288), OP.is_equal)
             quant("ml", view("ml", 1152 * al, 1152 * al + 4 * w), 288 * al, 288 * al + w)
             mm(1, w, "ob", 0, "ml", 288 * al, al == 4, al == 0)
             for a in aa:
-                i, o, acc = view("ml", 1152 * al + a % 4, 1152 * al + 64 * a, 4), view("dump", 288 * (a % 4), 288 * (a % 4) + 16 * a), view("rs", a, a + 1)
-                run("S", lambda: g.scalar.activation(o[6], i[6], ACT.Identity, bias=17.0, scale=-17.0, accum_out=acc[6]), [i], [o, acc])
+                if a:
+                    i, o, acc = view("ml", 1152 * al + a % 4, 1152 * al + 64 * a, 4), view("dump", 288 * (a % 4), 288 * (a % 4) + 16 * a), view("rs", a, a + 1)
+                    run("S", lambda: g.scalar.activation(o[6], i[6], ACT.Identity, bias=1.0, scale=-1.0, accum_out=acc[6]), [i], [o, acc])
         sr_rows(range(4, 8))
         if rnd == 0:
             constants_2()
@@ -307,17 +310,14 @@ def rank_program(g, core, T, topo):
             act(view("fw", 288 * k, 288 * k + 288), ps(2 + k % 4, 0, 288))
         for k, gr in enumerate((2, 3, 6, 7)):
             mm(2 + k, C, "up", 128 + 128 * gr, "x", 0)
-        tt(view("dm", 0, 288), ps(1, 0, 288), view("mk17", 0, 288), OP.mult)
-        r17 = view("r17", 0, 18)
-        tree("dm", r17)
-        tt(r17, r17, view("rs", 0, 18), OP.add)
-        ts(view("q32", 0, 18), r17, 1.0 / 289.0, OP.mult, -136.0 / 289.0, OP.add)
-        ts(view("qf", 0, 18), view("q32", 0, 18), -288.0, OP.mult)
-        tt(view("pof", 0, 18), r17, view("qf", 0, 18), OP.add)
-        tc(view("posl", 0, 18), view("pof", 0, 18))
+        tt(view("dm", 0, 288), ps(1, 0, 288), view("mk16", 0, 288), OP.mult)
+        sums(view("wm", 0, 288), view("kp16", 0, 288), view("dm", 0, 288))
+        rk = view("rk", 0, 18)
+        tt(rk, view("wm", 15, 288, 16), view("rs", 0, 18), OP.add)
+        tc(view("posl", 0, 18), rk)
         scatter(view("sort", 0, 288), view("posl", 0, 18), view("ssb", 0, 288))
         sm = view("spm", 0, 16)
-        tt(sm, view("sort", 272, 288), view("mk16", 0, 16), OP.mult)
+        tt(sm, view("sort", 16, 288, 17), view("mk16", 0, 16), OP.mult)
         sp, spa, dec = view("spv", 0, 1), view("spv", 1, 2), view("spv", 2, 3)
         run("V", lambda: g.vector.tensor_reduce(spa[6], sm[6], AxisListType.X, OP.add, apply_absolute_value=True), [sm], [spa])
         run("V", lambda: g.vector.tensor_reduce(sp[6], sm[6], AxisListType.X, OP.add), [sm], [sp])
@@ -325,15 +325,13 @@ def rank_program(g, core, T, topo):
         ts(view("sp8", 0, 8), view("neg8", 0, 8), dec, OP.mult, sp, OP.add)
         tt(view("sp8", 8, 16), view("sp8", 0, 8), view("own8", 0, 8), OP.add)
         ts(view("sp8", 16, 24), view("sp8", 8, 16), dec, OP.add)
-        runs = [lambda: tt(view("wm", 0, 272), view("sort", 0, 272), view("mk272", 0, 272), OP.mult),
-                lambda: tt(view("wm", 0, 136), view("wm", 0, 136), view("wm", 136, 272), OP.add),
-                lambda: tt(view("wm", 0, 68), view("wm", 0, 68), view("wm", 68, 136), OP.add),
-                lambda: tt(view("wm", 0, 34), view("wm", 0, 34), view("wm", 34, 68), OP.add),
-                lambda: tt(view("wn", 0, 17), view("wm", 0, 17), view("wm", 17, 34), OP.add),
-                lambda: [ts(view("wt", 0, 17), view("wn", 0, 17), EPS, OP.mult, -DELTA, OP.add),
-                         ts(view("wt", 24, 41), view("wn", 0, 17), -EPS, OP.mult, -DELTA, OP.add)],
+        v = view("wr", 15, 288, 17)
+        runs = [lambda: tt(view("wm", 0, 288), view("sort", 0, 288), view("mk17", 0, 288), OP.mult),
+                lambda: sums(view("wr", 0, 288), view("kp17", 0, 288), view("wm", 0, 288)),
+                lambda: [ts(view("wt", 0, 17), v, EPS, OP.mult, -DELTA, OP.add), ts(view("wt", 24, 41), v, -EPS, OP.mult, -DELTA, OP.add)],
+                lambda: tc(view("wn", 0, 17), v),
                 lambda: tt(view("wt", 48, 65), view("wt", 0, 17), view("wt", 24, 41), OP.min),
-                lambda: [tt(view("wn", 24, 41), view("wn", 0, 17), view("wt", 48, 65), OP.add), ts(view("rr", 0, 18), r17, 1.0 / 17.0, OP.mult)]]
+                lambda: tt(view("wn", 24, 41), v, view("wt", 48, 65), OP.add)]
         for gr in range(8):
             o, i = view("mc", 288 * gr, 288 * gr + 288), view("sr", 288 * gr, 288 * gr + 288)
             if gr % 4 >= 2:
@@ -342,7 +340,8 @@ def rank_program(g, core, T, topo):
                 act(o, s, ACT.Relu)
             else:
                 ts(o, i, view("sp8", 8 + gr, 9 + gr), OP.is_le)
-            runs[gr]()
+            if gr < 6:
+                runs[gr]()
             if gr % 4 == 3:
                 hf = gr // 4
                 quant("mc", view("mc", 1152 * hf, 1152 * hf + 1152), 288 * hf, 288 * hf + 288)
@@ -371,10 +370,9 @@ def rank_program(g, core, T, topo):
                 quant("mf", m, 144 * k, 144 * k + 144)
                 mm(1, H, "zz", 96 - 32 * k, "mf", 144 * k, False, k == 3)
         tt(view("wm", 0, 144), ps(1, 0, 144), view("mselt", 0, 144), OP.mult)
-        tt(view("d2", 0, 72), view("wm", 0, 72), view("wm", 72, 144), OP.add)
-        tt(view("d3", 0, 36), view("d2", 0, 72, 2), view("d2", 1, 72, 2), OP.add)
-        tt(view("pof", 0, 18), view("d3", 0, 36, 2), view("d3", 1, 36, 2), OP.add)
-        tt(view("nt", 0, 18), view("pof", 0, 18), view("rr", 0, 18), OP.add)
+        sums(view("nc", 0, 144), view("kp4", 0, 144), view("wm", 0, 144))
+        tt(view("pof", 0, 18), view("nc", 3, 72, 4), view("nc", 75, 144, 4), OP.add)
+        tt(view("nt", 0, 18), view("pof", 0, 18), rk, OP.add)
 
     def seats(rnd):
         n = view("nt", 0, 18)
@@ -391,8 +389,8 @@ def rank_program(g, core, T, topo):
         turn(view("itr", 0, 2304), iw)
         e = [(72 * k, 72 * k + 72) for k in range(7)]
         i0, i1 = view("itr", 0, 2304, 32), view("itr", 16, 2304, 32)
-        ts(view("en", *e[0]), i0, 0.0, OP.not_equal, pcol[3], OP.mult)
-        ts(view("en", *e[1]), i1, 0.0, OP.not_equal, pcol[4], OP.mult)
+        ts(view("en", *e[0]), i0, 0.0, OP.not_equal, pf[7], OP.mult)
+        ts(view("en", *e[1]), i1, 0.0, OP.not_equal, pf[8], OP.mult)
         tt(view("en", *e[2]), view("en", *e[0]), i0, OP.add)
         tt(view("en", *e[3]), view("en", *e[1]), i1, OP.add)
         tt(view("en", *e[4]), view("en", *e[2]), view("en", *e[3]), OP.add)
@@ -410,7 +408,7 @@ def rank_program(g, core, T, topo):
                 i = view(src, sc + n * q, sc + n * q + n, 1, 32 * t, 32 * t + 32)
             else:
                 i = view(src, sc + q, sc + 4 * n, 4, 32 * t, 32 * t + 32)
-            if k % 3 == 2:
+            if k % 8 in (2, 5, 6):
                 act(o, i)
             else:
                 tc(o, i)

from concourse.mybir import dt, AluOpType, AxisListType, ActivationFunctionType

OP = AluOpType
ACT = ActivationFunctionType
C = 288
H = 144
BIG = 1.0e29
EPS = 2.0 ** -24 + 2.0 ** -40
DELTA = 2.0 ** -100
MASKS = [1, 2, 3]

SCRATCH = {}
for _t, _s in (
        ("float32", "pf 16 gm 8 it0 320 it1 320 it2 320 neg8 8 own8 8 offadd 144 offt 144 offe 144 offo 144 msel 144 mselt 144 cvf 288 bigm 288 ssb 288 sst 288 sr 2304 dm 288 sc 288 rs 18 rk 18 pof 18 nc 144 sort 288 spm 16 spv 4 sp8 24 wm 288 wr 288 wn 72 wt 72 off32 144 off33 144 ntf 32 ntt 32 en 504 rt 1152"),
        ("int32", "pi 8 ii 256 nt 32 ph 96"),
        ("uint16", "clist 18 ul 72 wl 64 posl 18 off 144 phl 18 tl 72 hl 72"),
        ("bfloat16", "dump 1152 mk16 288 mk17 288 kp16 288 kp17 288 kp4 144 cval 288 ones 64 zer 2304 ef 4096 ob 512 zb 1024 zz 1792 xt 1152 ut 512 vt 512 ml 5760 mc 2304 mf 2304 iw0 2304 iw1 2304 iw2 2304 itr 2304 fw 2304 ow 1152 tt 1152 o2 1152 tw 2304"),
        ("mx", "ef 1024 ob 128 zb 256 zz 448 u 128 v 128 up 1152 w 512 wl 1024 x 288 ml 1440 mc 576 mf 576 tb 144 ta0 144 ta1 144 ta2 144 lc0 144 lc1 144 lc2 144")):
    _s = _s.split()
    for _n, _w in zip(_s[::2], _s[1::2]):
        if _t == "mx":
            SCRATCH[_n + "_q"] = ("sbuf", [128, int(_w)], "float8_e4m3fn_x4")
            SCRATCH[_n + "_s"] = ("sbuf", [128, int(_w)], "uint8")
        else:
            SCRATCH[_n] = ("sbuf", [128, int(_w)], _t)
for _m in range(8):
    SCRATCH["p%d" % _m] = ("psum", [128, 512], "float32")

SEMAPHORES = "sv sa st sg lx lu lw ls lv z0 z1 z2 z3 z4 z5 z6 outd arr0 arr1 arr2 sent0 sent1 sent2".split()


def rank_program(g, core, T, topo):
    rank = T.rank_of(core)
    if rank is None:
        return
    wait = {"V": g.vector.wait_ge, "S": g.scalar.wait_ge, "T": g.tensor.wait_ge, "G": g.wait_ge, "Y": g.sync.wait_ge}
    own = {"V": "sv", "S": "sa", "T": "st", "G": "sg"}
    total, snaps, hist = {}, {}, {}
    known = {q: {} for q in "VSTGYR"}

    def view(name, c0, c1, st=1, p0=0, p1=128):
        if p0 == 0 and p1 == 128:
            ap = T[name][:, c0:c1] if st == 1 else T[name][:, c0:c1:st]
        else:
            ap = T[name][p0:p1, c0:c1] if st == 1 else T[name][p0:p1, c0:c1:st]
        return (name, p0, p1, c0, c1, st, ap)

    def clash(a, b):
        if a[1] >= b[2] or b[1] >= a[2] or a[3] >= b[4] or b[3] >= a[4]:
            return False
        return not (a[5] == b[5] and a[5] > 1 and (a[3] - b[3]) % a[5])

    def covers(a, b):
        return a[1] <= b[1] and a[2] >= b[2] and a[3] <= b[3] and a[4] >= b[4] and (a[5] == 1 or (a[5] == b[5] and (a[3] - b[3]) % a[5] == 0))

    def settle(q, reads, writes, group=False):
        need = {}
        for kind, vs in (("r", reads), ("w", writes)):
            for v in vs:
                bank = SCRATCH[v[0]][0] == "psum"
                for (k2, q2, v2, sem, val) in hist.get(v[0], []):
                    if q2 == q and q in "VSTG":
                        if (kind == "r" and k2 == "r") or (group and bank) or not clash(v, v2):
                            continue
                    elif not bank and ((kind == "r" and k2 == "r") or not clash(v, v2)):
                        continue
                    need[sem] = max(need.get(sem, 0), val)
        kn = known[q]
        for sem, val in sorted(need.items(), key=lambda e: -e[1]):
            if kn.get(sem, 0) >= val:
                continue
            wait[q](T.sem[sem], val)
            kn[sem] = val
            for s2, v2 in snaps.get((sem, val), {}).items():
                kn[s2] = max(kn.get(s2, 0), v2)

    def note(q, sem, val, reads, writes):
        snaps[(sem, val)] = dict(known[q])
        for k, vs in (("w", writes), ("r", reads)):
            for v in vs:
                h = hist.setdefault(v[0], [])
                if k == "w":
                    h[:] = [e for e in h if not covers(v, e[2])]
                else:
                    h[:] = [e for e in h if not (e[0] == "r" and e[1] == q and q in "VSTG" and covers(v, e[2]))]
                h.append((k, q, v, sem, val))

    def run(q, call, reads, writes, group=False):
        settle(q, reads, writes, group)
        sem = own[q]
        total[sem] = total.get(sem, 0) + 1
        call().then_inc(T.sem[sem], 1)
        note(q, sem, total[sem], reads, writes)

    def dma(sem, out, in_, reads, writes):
        settle("Y", reads, writes)
        total[sem] = total.get(sem, 0) + 16
        g.sync.dma_start(out, in_).then_inc(T.sem[sem], 16)
        note("Y", sem, total[sem], reads, writes)

    def ap(x):
        return x[6] if isinstance(x, tuple) else x

    def rd(*xs):
        return [x for x in xs if isinstance(x, tuple)]

    def ts(out, a, s1, op0, s2=None, op1=None):
        if op1 is None:
            run("V", lambda: g.vector.tensor_scalar(out[6], a[6], ap(s1), None, op0), rd(a, s1), [out])
        else:
            run("V", lambda: g.vector.tensor_scalar(out[6], a[6], ap(s1), ap(s2), op0, op1), rd(a, s1, s2), [out])

    def tt(out, a, b, op):
        run("V", lambda: g.vector.tensor_tensor(out[6], a[6], b[6], op), [a, b], [out])

    def tc(out, a):
        run("V", lambda: g.vector.tensor_copy(out[6], a[6]), [a], [out])

    def fill(out, c):
        run("V", lambda: g.vector.memset(out[6], c), [], [out])

    def sums(out, keep, a):
        run("V", lambda: g.vector.tensor_tensor_scan(out[6], keep[6], a[6], 0.0, OP.mult, OP.add), [keep, a], [out])

    def fetch(out, win, off):
        run("S", lambda: g.scalar.activation(out[6], win[6].indirect(off[6]), ACT.Copy), [win, off], [out])

    def gather2(out, c0, win, off, o0, n):
        m = n // 2
        a, e = view(out, c0, c0 + 16 * m), view(off, o0, o0 + m)
        run("V", lambda: g.vector.tensor_copy(a[6], win[6].indirect(e[6])), [win, e], [a])
        fetch(view(out, c0 + 16 * m, c0 + 16 * n), win, view(off, o0 + m, o0 + n))

    def fused(out, win, off, b, op):
        run("V", lambda: g.vector.tensor_tensor(out[6], win[6].indirect(off[6]), b[6], op), [win, off, b], [out])

    def scatter(win, off, a):
        run("V", lambda: g.vector.tensor_copy(win[6].indirect(off[6]), a[6]), [a, off], [win])

    def turn(out, a):
        run("V", lambda: g.vector.transpose(out[6], a[6]), [a], [out])

    def quant(n, a, c0, c1):
        o, p = view(n + "_q", c0, c1), view(n + "_s", c0, c1)
        run("V", lambda: g.vector.quantize_mx(o[6], p[6], a[6]), [a], [o, p])

    def act(out, a, f=ACT.Copy, scale=1.0, bias=0.0):
        if isinstance(scale, tuple):
            run("S", lambda: g.scalar.activation(out[6], a[6], f, scale=scale[6]), [a, scale], [out])
        elif bias:
            run("S", lambda: g.scalar.activation(out[6], a[6], ACT.Identity, bias=bias, scale=scale), [a], [out])
        elif scale == 1.0:
            run("S", lambda: g.scalar.activation(out[6], a[6], f), [a], [out])
        else:
            run("S", lambda: g.scalar.activation(out[6], a[6], f, scale=scale), [a], [out])

    def iota(out, pattern, base=0, cm=0, f=True):
        if f:
            run("G", lambda: g.iota(out[6], pattern, base, cm, allow_small_or_imprecise_dtypes=True), [], [out])
        else:
            run("G", lambda: g.iota(out[6], pattern, base, cm), [], [out])

    def mm(bank, n, l, l0, r, r0, start=True, stop=True):
        o = view("p%d" % bank, 0, n)
        lq, ls, rq, rs = view(l + "_q", l0, l0 + 128), view(l + "_s", l0, l0 + 128), view(r + "_q", r0, r0 + n), view(r + "_s", r0, r0 + n)
        run("T", lambda: g.tensor.matmul_mx(o[6], lq[6], ls[6], rq[6], rs[6], start, stop), [lq, ls, rq, rs], [o], group=not start)

    def ps(bank, c0, c1, st=1):
        return view("p%d" % bank, c0, c1, st)

    def pick(dst, src, n0, n1, w, off):
        o, i, o2, i2 = view(dst + "_q", n0, n1), view(src + "_q", 0, w), view(dst + "_s", n0, n1), view(src + "_s", 0, w)
        run("V", lambda: g.vector.tensor_copy(o[6].bitcast(dt.uint32), i[6].bitcast(dt.uint32).indirect(off[6])), [i, off], [o])
        fetch(o2, i2, off)

    for sem, name, src, w in (("lx", "xt", T.x, 1152), ("lu", "ut", T.u, 512)):
        dma(sem, T[name][:, 0:w], src[:], [], [view(name, 0, w)])
    dma("lw", T.w_q[:, 0:512].bitcast(dt.uint8), T.wc[:], [], [view("w_q", 0, 512)])
    dma("ls", T.w_s[:, 0:512], T.ws[:], [], [view("w_s", 0, 512)])
    dma("lv", T.vt[:, 0:512], T.v[:], [], [view("vt", 0, 512)])
    pf = [view("pf", k, k + 1) for k in range(11)]
    kappa, group, parity, kap4 = pf[1], pf[2], pf[3], pf[5]
    pi = [view("pi", k, k + 1) for k in range(8)]
    iota(pi[0], [[0, 1]], 0, 1, f=False)
    iota(view("ii", 0, 8), [[16, 8]], f=False)
    iota(view("ii", 8, 72), [[16, 8], [0, 8]], f=False)
    iota(view("it0", 0, 288), [[0, 18], [1, 16]])
    iota(view("it1", 144, 152), [[1, 8]])
    iota(view("ii", 72, 90), [[16, 18]], 15, 0, f=False)
    iota(view("it1", 0, 144), [[1, 8], [0, 18]])
    iota(view("it2", 0, 289), [[0, 17], [1, 17]])
    iota(view("cvf", 0, 288), [[1, 288]], -144, 0)
    iota(view("it1", 160, 304), [[0, 36], [1, 4]])
    iota(view("ii", 96, 160), [[16, 8], [128, 4], [0, 2]], f=False)

    fill(view("zer", 0, 2304), 0.0)
    for sem, name, c0, c1 in (("z0", "ef", 0, 2304), ("z1", "ef", 2304, 4096), ("z5", "zb", 0, 1024), ("z6", "zz", 0, 1792), ("z2", "iw0", 0, 2304), ("z3", "iw1", 0, 2304), ("z4", "iw2", 0, 2304)):
        dma(sem, T[name][:, c0:c1], T.zer[:, 0:c1 - c0], [view("zer", 0, c1 - c0)], [view(name, c0, c1)])
    fill(view("ones", 0, 64), 1.0)
    fill(view("rs", 0, 1), 0.0)
    act(view("ml", 0, 512), view("zer", 0, 512))
    act(view("ml", 1152, 1664), view("zer", 0, 512))
    for al, b, c, w in ((2, 0, 144, 192), (2, 1, 160, 192), (2, 2, 176, 192), (3, 0, 208, 256), (3, 1, 224, 256), (3, 2, 240, 256), (4, 0, 272, 288), (4, 3, 0, 288)):
        act(view("ml", 1152 * al + 4 * c + b, 1152 * al + 4 * w, 4), view("zer", 0, w - c))
    tc(view("ul", 0, 72), view("ii", 0, 72))
    ts(pi[1], pi[0], 15, OP.bitwise_and)
    ts(pi[2], pi[0], 4, OP.logical_shift_right)
    ts(pi[3], pi[0], 4, OP.logical_shift_right, 1, OP.bitwise_and)
    ts(pi[4], pi[0], 5, OP.logical_shift_right)
    ts(pi[5], pi[0], 15, OP.bitwise_and, 2, OP.logical_shift_right)
    ts(pi[6], pi[0], 4, OP.bitwise_and, 2, OP.logical_shift_right)
    tc(view("pf", 0, 7), view("pi", 0, 7))
    act(pf[7], pf[4], ACT.Identity, 576.0, 144.0)
    act(pf[8], pf[4], ACT.Identity, 576.0, 432.0)
    act(pf[9], pf[6], ACT.Copy, 4096.0)
    act(pf[10], pf[6], ACT.Identity, -4096.0, 4096.0)
    ts(view("mk16", 0, 288), view("it0", 0, 288), kappa, OP.is_equal)
    ts(view("kp16", 0, 288), view("it0", 0, 288), 0.0, OP.not_equal)
    ts(view("gm", 0, 8), view("it1", 144, 152), group, OP.is_equal)
    for h in range(8):
        for t in range(4):
            o, i = view("ef", 512 * h + 128 * t + t, 512 * h + 128 * t + 128, 4), view("ones", 0, 32)
            run("G", lambda: g.affine_select(o[6], i[6], [[0, 2], [-1, 16]], OP.is_equal, 0.0, -16 * h, 1), [i], [o])
    quant("u", view("ut", 0, 512), 0, 128)
    pick("up", "u", 0, 128, 128, view("ul", 0, 8))

    def constants_0():
        ts(view("bigm", 0, 288), view("it0", 0, 288), kappa, OP.is_le, BIG, OP.mult)
        tc(view("clist", 0, 18), view("ii", 72, 90))

    def constants_1():
        pick("up", "u", 128, 1152, 128, view("ul", 8, 72))
        for k in range(8):
            act(view("ob", 64 * k, 64 * k + 64), view("ones", 0, 64), ACT.Copy, view("gm", k, k + 1))
        quant("ob", view("ob", 0, 512), 0, 128)
        for z in range(4):
            for b in range(4):
                act(view("zb", 512 * (z // 2) + 16 * z + 5 * b, 512 * (z // 2) + 512, 64), view("gm", 0, 8))

    def constants_2():
        for w in range(2):
            for b in range(4):
                act(view("zz", 896 * w + 384 + 5 * b, 896 * w + 512, 16), view("ones", 0, 8), ACT.Copy, 16.0 if w else 1.0)
        act(view("cval", 0, 288), view("cvf", 0, 288))
        ts(view("neg8", 0, 8), view("it1", 144, 152), group, OP.is_lt, -1.0, OP.mult)
        ts(view("own8", 0, 8), view("it1", 144, 152), group, OP.is_equal, -BIG, OP.mult)
        ts(view("offadd", 0, 144), view("it1", 0, 144), group, OP.is_lt, 24.0, OP.mult)
        ts(view("offt", 0, 144), view("it1", 0, 144), group, OP.is_equal, 48.0, OP.mult)
        ts(view("kp17", 0, 288), view("it2", 0, 288), 0.0, OP.not_equal)
        tt(view("offadd", 0, 144), view("offadd", 0, 144), view("offt", 0, 144), OP.add)
        ts(view("kp4", 0, 144), view("it1", 160, 304), 0.0, OP.not_equal)
        ts(view("offe", 0, 144), view("offadd", 0, 144), pf[9], OP.subtract)
        ts(view("offo", 0, 144), view("offadd", 0, 144), pf[10], OP.subtract)
        ts(view("mk17", 0, 288), view("it2", 0, 288), kappa, OP.is_equal)
        fill(view("wn", 0, 48), 0.0)
        fill(view("wn", 48, 72), -BIG)
        ts(view("msel", 0, 144), view("it1", 160, 304), kap4, OP.is_equal)
        ts(view("mselt", 0, 144), view("msel", 0, 144), parity, OP.mult)
        quant("ef", view("ef", 0, 2048), 0, 512)
        tt(view("mselt", 0, 72), view("msel", 0, 72), view("mselt", 0, 72), OP.subtract)
        quant("ef", view("ef", 2048, 4096), 512, 1024)
        quant("zb", view("zb", 0, 1024), 0, 256)
        quant("zz", view("zz", 0, 1792), 0, 448)
        fill(view("cval", 144, 145), 0.25)

    def constants_3():
        ts(view("ii", 160, 224), view("ii", 96, 160), kappa, OP.add)
        tc(view("wl", 0, 64), view("ii", 160, 224))
        pick("wl", "w", 0, 1024, 512, view("wl", 0, 64))
        quant("v", view("vt", 0, 512), 0, 128)

    def places(rnd):
        mm(0, C, "up", 0, "x", 0)
        if rnd == 0:
            constants_0()
        tt(view("dm", 0, 288), ps(0, 0, 288), view("mk16", 0, 288), OP.mult)
        tc(view("ssb", 0, 288), ps(0, 0, 288))
        sums(view("sc", 0, 288), view("kp16", 0, 288), view("dm", 0, 288))
        tt(view("sst", 0, 288), ps(0, 0, 288), view("bigm", 0, 288), OP.add)
        if rnd == 0:
            constants_1()

        def sr_rows(ks):
            for k in ks:
                act(view("sr", 288 * k, 288 * k + 288), ps(2 + k % 4, 0, 288))

        for k in range(4):
            mm(2 + k % 4, C, "up", 128 + 128 * k, "x", 0)
        sr_rows(range(4))
        for k in range(4, 8):
            mm(2 + k % 4, C, "up", 128 + 128 * k, "x", 0)
        for al in (4, 3, 2, 1, 0):
            w = C if al == 4 else max(128, 64 * al + 64)
            aa = range(4 * al, min(18, 4 * al + 4))
            for a in aa:
                ts(view("ml", 1152 * al + a % 4, 1152 * al + 64 * a + 64, 4), view("ssb", 0, 16 * a + 16), view("sc", 16 * a + 15, 16 * a + 16), OP.is_lt)
            if al == 4:
                fused(view("ml", 4 * 1152 + 2, 5760, 4), view("sc", 0, 288), view("clist", 0, 18), view("sst", 0, 288), OP.is_equal)
            quant("ml", view("ml", 1152 * al, 1152 * al + 4 * w), 288 * al, 288 * al + w)
            mm(1, w, "ob", 0, "ml", 288 * al, al == 4, al == 0)
            for a in aa:
                if a:
                    i, o, acc = view("ml", 1152 * al + a % 4, 1152 * al + 64 * a, 4), view("dump", 288 * (a % 4), 288 * (a % 4) + 16 * a), view("rs", a, a + 1)
                    run("S", lambda: g.scalar.activation(o[6], i[6], ACT.Identity, bias=1.0, scale=-1.0, accum_out=acc[6]), [i], [o, acc])
        sr_rows(range(4, 8))
        if rnd == 0:
            constants_2()
        for k in range(8):
            mm(2 + k % 4, C, "ef", 128 * k, "x", 0)
            act(view("fw", 288 * k, 288 * k + 288), ps(2 + k % 4, 0, 288))
        for k, gr in enumerate((2, 3, 6, 7)):
            mm(2 + k, C, "up", 128 + 128 * gr, "x", 0)
        tt(view("dm", 0, 288), ps(1, 0, 288), view("mk16", 0, 288), OP.mult)
        sums(view("wm", 0, 288), view("kp16", 0, 288), view("dm", 0, 288))
        rk = view("rk", 0, 18)
        tt(rk, view("wm", 15, 288, 16), view("rs", 0, 18), OP.add)
        tc(view("posl", 0, 18), rk)
        scatter(view("sort", 0, 288), view("posl", 0, 18), view("ssb", 0, 288))
        sm = view("spm", 0, 16)
        tt(sm, view("sort", 16, 288, 17), view("mk16", 0, 16), OP.mult)
        sp, spa, dec = view("spv", 0, 1), view("spv", 1, 2), view("spv", 2, 3)
        run("V", lambda: g.vector.tensor_reduce(spa[6], sm[6], AxisListType.X, OP.add, apply_absolute_value=True), [sm], [spa])
        run("V", lambda: g.vector.tensor_reduce(sp[6], sm[6], AxisListType.X, OP.add), [sm], [sp])
        ts(dec, spa, EPS, OP.mult, DELTA, OP.add)
        ts(view("sp8", 0, 8), view("neg8", 0, 8), dec, OP.mult, sp, OP.add)
        tt(view("sp8", 8, 16), view("sp8", 0, 8), view("own8", 0, 8), OP.add)
        ts(view("sp8", 16, 24), view("sp8", 8, 16), dec, OP.add)
        v = view("wr", 15, 288, 17)
        runs = [lambda: tt(view("wm", 0, 288), view("sort", 0, 288), view("mk17", 0, 288), OP.mult),
                lambda: sums(view("wr", 0, 288), view("kp17", 0, 288), view("wm", 0, 288)),
                lambda: [ts(view("wt", 0, 17), v, EPS, OP.mult, -DELTA, OP.add), ts(view("wt", 24, 41), v, -EPS, OP.mult, -DELTA, OP.add)],
                lambda: tc(view("wn", 0, 17), v),
                lambda: tt(view("wt", 48, 65), view("wt", 0, 17), view("wt", 24, 41), OP.min),
                lambda: tt(view("wn", 24, 41), v, view("wt", 48, 65), OP.add)]
        for gr in range(8):
            o, i = view("mc", 288 * gr, 288 * gr + 288), view("sr", 288 * gr, 288 * gr + 288)
            if gr % 4 >= 2:
                s, b = view("dump", 288 * (gr % 4), 288 * (gr % 4) + 288), view("sp8", 16 + gr, 17 + gr)
                run("S", lambda: g.scalar.activation(s[6], i[6], ACT.Sign, bias=b[6], scale=-1.0), [i, b], [s])
                act(o, s, ACT.Relu)
            else:
                ts(o, i, view("sp8", 8 + gr, 9 + gr), OP.is_le)
            if gr < 6:
                runs[gr]()
            if gr % 4 == 3:
                hf = gr // 4
                quant("mc", view("mc", 1152 * hf, 1152 * hf + 1152), 288 * hf, 288 * hf + 288)
                for z in range(2):
                    mm(6 + hf, 286, "zb", 128 * z, "mc", 288 * hf + 2 * z, z == 0, z == 1)
        for k in range(4):
            for w in range(2):
                mm(1, H, "zz", 224 * w + 96 - 32 * k, "mc", 144 * k, k == 0 and w == 0, False)
        for hf in range(2):
            c0, c1 = 72 * hf, 72 * hf + 72
            o, o2 = view("off32", c0, c1), view("off33", c0, c1)
            tt(o, ps(6 + hf, 0, 286, 4), view("offe", c0, c1), OP.add)
            tt(o2, ps(6 + hf, 1, 286, 4), view("offo", c0, c1), OP.add)
            tt(o, o, o2, OP.max)
            tc(view("off", c0, c1), o)
            w = view("wn", 0, 72)
            fetch(view("rt", 576 * hf, 576 * hf + 576), w, view("off", c0 + 36, c1))
            for k in (2 * hf, 2 * hf + 1):
                m = view("mf", 576 * k, 576 * k + 576)
                if k % 2 == 0:
                    fused(m, w, view("off", 36 * k, 36 * k + 36), view("sr", 576 * k, 576 * k + 576), OP.is_ge)
                else:
                    for e in range(2):
                        c = 576 * hf + 288 * e
                        tt(view("mf", 576 * k + 288 * e, 576 * k + 288 * e + 288), view("rt", c, c + 288), ps(2 + 2 * hf + e, 0, 288), OP.is_ge)
                quant("mf", m, 144 * k, 144 * k + 144)
                mm(1, H, "zz", 96 - 32 * k, "mf", 144 * k, False, k == 3)
        tt(view("wm", 0, 144), ps(1, 0, 144), view("mselt", 0, 144), OP.mult)
        sums(view("nc", 0, 144), view("kp4", 0, 144), view("wm", 0, 144))
        tt(view("pof", 0, 18), view("nc", 3, 72, 4), view("nc", 75, 144, 4), OP.add)
        tt(view("nt", 0, 18), view("pof", 0, 18), rk, OP.add)

    def seats(rnd):
        n = view("nt", 0, 18)
        ph = [view("ph", 18 * k, 18 * k + 18) for k in range(5)]
        ts(ph[0], n, 1, OP.logical_shift_right)
        ts(ph[1], n, 1, OP.logical_shift_right, 65520, OP.bitwise_and)
        ts(ph[2], n, 16, OP.mult)
        ts(ph[3], ph[0], -31, OP.mult)
        tt(ph[2], ph[2], ph[1], OP.add)
        tt(ph[4], ph[2], ph[3], OP.add)
        tc(view("phl", 0, 18), ph[4])
        iw = view("iw%d" % rnd, 0, 2304)
        scatter(iw, view("phl", 0, 18), view("cval", 0, 288))
        turn(view("itr", 0, 2304), iw)
        e = [(72 * k, 72 * k + 72) for k in range(7)]
        i0, i1 = view("itr", 0, 2304, 32), view("itr", 16, 2304, 32)
        ts(view("en", *e[0]), i0, 0.0, OP.not_equal, pf[7], OP.mult)
        ts(view("en", *e[1]), i1, 0.0, OP.not_equal, pf[8], OP.mult)
        tt(view("en", *e[2]), view("en", *e[0]), i0, OP.add)
        tt(view("en", *e[3]), view("en", *e[1]), i1, OP.add)
        tt(view("en", *e[4]), view("en", *e[2]), view("en", *e[3]), OP.add)
        tc(view("en", *e[5], p1=64), view("en", *e[4], p0=64))
        tt(view("en", *e[6], p1=64), view("en", *e[4], p1=64), view("en", *e[5], p1=64), OP.add)
        tc(view("en", *e[0], p1=32), view("en", *e[6], p0=32, p1=64))
        tt(view("en", *e[1], p1=32), view("en", *e[6], p1=32), view("en", *e[0], p1=32), OP.add)
        for t in range(4):
            tc(view("tl", 0, 72, p0=32 * t, p1=32 * t + 32), view("en", *e[1], p1=32))

    def native(dst, dc, src, sc, n, sst, order):
        for k, (q, t) in enumerate(order):
            o = view(dst, dc + t, dc + 4 * n, 4, 32 * q, 32 * q + 32)
            if sst == 1:
                i = view(src, sc + n * q, sc + n * q + n, 1, 32 * t, 32 * t + 32)
            else:
                i = view(src, sc + q, sc + 4 * n, 4, 32 * t, 32 * t + 32)
            if k % 8 in (2, 5, 6):
                act(o, i)
            else:
                tc(o, i)

    ALL = [(q, t) for q in range(4) for t in range(4)]

    def layer(src, half):
        for h in range(8):
            a, b = (2 * h) % 8, (2 * h + 1) % 8
            mm(a, H, "wl", 128 * h, src, 0)
            mm(b, H, "ef", 128 * h, src, 0)
            r = view("rt", 144 * h, 144 * h + 144)
            act(r, ps(a, 0, 144), ACT.Relu, 0.03125)
            tt(view("tw", 1152 * half + h, 1152 * half + 1152, 8), ps(b, 0, 144), r, OP.add)

    for rnd in range(3):
        quant("x", view("xt", 0, 1152), 0, 288)
        places(rnd)
        seats(rnd)
        ta, lc = "ta%d" % rnd, "lc%d" % rnd
        gather2("ow", 0, view("fw", 0, 2304), "tl", 0, 36)
        native("tt", 0, "ow", 0, 144, 4, ALL)
        quant(ta, view("tt", 0, 576), 0, 144)
        dst = T.cores[rank ^ MASKS[rnd]]
        rid, pid = topo.addr(dst)[0], topo.addr(dst)[1]
        mask, ne = topo.mask(core, dst), len(topo.engines(core, dst))
        settle("G", [view(ta + "_q", 0, 144), view(ta + "_s", 0, 144)], [])
        arr, sent = "arr%d" % rnd, "sent%d" % rnd
        g.remote_dma(T[lc + "_q"][:, 0:144].bitcast(dt.uint8), T[ta + "_q"][:, 0:144].bitcast(dt.uint8), T.sem[arr], T.sem[sent], pid, rid, mask)
        g.remote_dma(T[lc + "_s"][:, 0:144], T[ta + "_s"][:, 0:144], T.sem[arr], T.sem[sent], pid, rid, mask)
        total[arr] = total[sent] = 2 * ne
        note("R", arr, 2 * ne, [], [view(lc + "_q", 0, 144), view(lc + "_s", 0, 144)])
        gather2("ow", 576, view("fw", 0, 2304), "tl", 36, 36)
        native("tt", 576, "ow", 576, 144, 4, ALL)
        quant("tb", view("tt", 576, 1152), 0, 144)
        if rnd == 0:
            constants_3()
        for q in range(4):
            tc(view("hl", 18 * q, 18 * q + 18, p1=32), view("nt", 0, 18, p0=32 * q, p1=32 * q + 32))
        for t in range(1, 4):
            tc(view("hl", 0, 72, p0=32 * t, p1=32 * t + 32), view("hl", 0, 72, p1=32))
        layer("tb", 1)
        if rnd == 2:
            fill(view("ntf", 18, 32), 0.0)
            tc(view("ntf", 0, 18), view("nt", 0, 18))
            turn(view("ntt", 0, 32), view("ntf", 0, 32))
            for gr in range(8):
                v = view("ntt", 16 * (gr % 2), 16 * (gr % 2) + 16, 1, 32 * (gr // 2), 32 * (gr // 2) + 18)
                dma("outd", T.pl[gr:gr + 1, :], v[6], [v], [])
        layer(lc, 0)
        for k in range(2):
            gather2("o2", 576 * k, view("tw", 0, 2304), "hl", 36 * k, 36)
            native("xt", 0, "o2", 0, 288, 1, ALL[8 * k:8 * k + 8])
    quant("x", view("xt", 0, 1152), 0, 288)
    mm(0, C, "v", 0, "x", 0)
    v = view("x_q", 0, 288)
    dma("outd", T.oc[:], v[6].bitcast(dt.uint8), [v], [])
    for k in range(4):
        v = view("x_s", 0, 288, 1, 32 * k, 32 * k + 4)
        dma("outd", T.osc[4 * k:4 * k + 4, :], v[6], [v], [])
    tc(view("dm", 0, 288), ps(0, 0, 288))
    v = view("dm", 0, 288)
    dma("outd", T.y[:], v[6], [v], [])
    for sem in SEMAPHORES:
        if known["G"].get(sem, 0) < total[sem]:
            g.wait_ge(T.sem[sem], total[sem])
